import numpy as np
import ml_dtypes


def mxq(x, axis, fmt="e4m3"):
    dtype, down = {"e4m3": (ml_dtypes.float8_e4m3fn, 7), "e5m2": (ml_dtypes.float8_e5m2, 14)}[fmt]
    v = np.moveaxis(np.asarray(x, np.float32).astype(ml_dtypes.bfloat16).astype(np.float64), axis, -1)
    blocks = v.reshape(v.shape[:-1] + (-1, 32))
    amax = np.abs(blocks).max(-1, keepdims=True)
    byte = np.maximum(np.where(amax > 0, np.frexp(amax)[1] - 1 + 127, 0) - down, 1)
    scale = np.exp2(byte - 127.0)
    codes = (blocks / scale).astype(np.float32).astype(dtype).astype(np.float64)
    return np.moveaxis((codes * scale).reshape(v.shape), -1, axis)


WIDE = False


def mx_kscale(k):
    if not WIDE:
        return np.ones(k)
    levels = np.array([10, -10, 5, -5, 0])
    if k % 512:
        return np.exp2(np.random.permutation(np.resize(levels, k // 32))).repeat(32)
    a = np.empty((k // 512, 16))
    for p in range(k // 512):
        a[p, :8] = np.random.permutation(np.resize(levels, 8))
        for g in range(8):
            far = levels[np.abs(levels - a[p, g]) >= 10]
            a[p, g + 8] = far[np.random.randint(len(far))]
    return np.exp2(a.ravel()).repeat(32)


def f64(x):
    return np.asarray(x).astype(np.float64)


def striped(idx):
    return np.tile(np.asarray(idx).reshape(-1, 16).T, (8, 1)).astype(np.uint16)


def unstriped(offs):
    return offs[:16].T.reshape(-1).astype(np.int64)


E2M1 = np.array([0.0, 0.5, 1.0, 1.5, 2.0, 3.0, 4.0, 6.0, -0.0, -0.5, -1.0, -1.5, -2.0, -3.0, -4.0, -6.0])


def pack_weight(w, fmt):
    k, n = w.shape
    w = f64(np.asarray(w, np.float32).astype(ml_dtypes.bfloat16)).reshape(k // 32, 32, n)
    amax = np.abs(w).max(1)
    if fmt == "e4m3":
        byte = np.frexp(amax)[1] - 1 + 127 - 7
    else:
        mant, ex = np.frexp(amax / 6.0)
        byte = np.where(mant > 0.5, ex, ex - 1) + 127
    byte = np.clip(np.where(amax > 0, byte, 1), 1, 254)
    scaled = (w * np.exp2(127.0 - byte)[:, None, :]).reshape(k, n).astype(np.float32)
    by_word = np.ascontiguousarray(scaled.reshape(k // 512, 128, 4, n).transpose(0, 1, 3, 2))
    if fmt == "e4m3":
        words = by_word.astype(ml_dtypes.float8_e4m3fn).view(np.uint8)
    else:
        c = by_word.astype(ml_dtypes.float4_e2m1fn).view(np.uint8) & 0xF
        words = (c[..., 0::2] | (c[..., 1::2] << 4)).reshape(k // 512, 128, 2 * n)
    return np.ascontiguousarray(words), np.ascontiguousarray(byte.astype(np.uint8).reshape(k // 512, 16, n))


def unpack_weight(words, scales, fmt):
    g, _, n = scales.shape
    words = np.ascontiguousarray(words).reshape(g, 128, n, -1)
    if fmt == "e4m3":
        vals = words.view(ml_dtypes.float8_e4m3fn).astype(np.float64)
    else:
        nib = np.empty((g, 128, n, 4), np.uint8)
        nib[..., 0::2] = words & 0xF
        nib[..., 1::2] = words >> 4
        vals = E2M1[nib]
    vals = vals * np.repeat(np.exp2(scales.astype(np.float64) - 127.0), 8, axis=1)[..., None]
    return vals.transpose(0, 1, 3, 2).reshape(g * 512, n)


B, N, T, D, NQ = 1, 512, 2048, 1024, 256


def setup_inputs():
    n = np.random.standard_normal
    pages = np.random.permutation(T // 16)[:B * N // 16]
    idx = (pages[:, None] * 16 + np.arange(16)[None, :]).reshape(-1)
    s = mx_kscale(D)[:, None]
    kp = pack_weight(n((D, T)) / s, "e2m1")
    return {
        "qT": (n((B, D, NQ)) * s * (8.00 / np.sqrt(D))).astype(np.float32),
        "k_words": np.ascontiguousarray(kp[0].reshape(1, 2, 128, T, 2).transpose(0, 2, 3, 1, 4)).reshape(1, 128, T, 4),
        "k_scales": kp[1],
        "kb": np.tile(n(2048), (128, 1)).astype(np.float32),
        "offs": striped(idx),
    }


def reference(qT, k_words, k_scales, kb, offs):
    idx = unstriped(offs)
    pick = lambda x, which: x[:, which].reshape(x.shape[0], B, -1).transpose(1, 0, 2)
    k = unpack_weight(k_words.reshape(1, 128, T, 2, 2).transpose(0, 3, 1, 2, 4).reshape(2, 128, 2 * T), k_scales, "e2m1")
    kg = pick(k, idx)
    qq = mxq(f64(qT), 1, "e4m3")
    a = qq.transpose(0, 2, 1) @ kg
    y = 30.0 * np.tanh(a / 30.0) + pick(f64(kb), idx)[:, :1, :]
    return y

@@ -1,0 +1,140 @@
+from contextlib import ExitStack
+
+import concourse.mybir as mybir
+from concourse.masks import make_identity
+
+F32 = mybir.dt.float32
+BF16 = mybir.dt.bfloat16
+I32 = mybir.dt.int32
+U32 = mybir.dt.uint32
+U16 = mybir.dt.uint16
+U8 = mybir.dt.uint8
+FP8X4 = mybir.dt.float8_e4m3fn_x4
+FP4X4 = mybir.dt.float4_e2m1fn_x4
+TANH = mybir.ActivationFunctionType.Tanh
+MULT = mybir.AluOpType.mult
+ADD = mybir.AluOpType.add
+
+P = 128
+PACK = 4
+SLOTS = 512
+TOKENS = 2048
+FEATURES = 1024
+QUERIES = 256
+CAP = 30.0
+SHIFT = 16
+BIAS_ROW = 8
+CHUNK = 256
+
+FLOPS = 2 * FEATURES * QUERIES * SLOTS
+BYTES = 4 * FEATURES * QUERIES + 4 * P * TOKENS + 32 * TOKENS + 4 * TOKENS + 2 * P * SLOTS // 16 + 4 * QUERIES * SLOTS
+
+
+def tile_attend_capkb_kernel(tc, qT, k_words, k_scales, kb, offs, out):
+    nc = tc.nc
+    with ExitStack() as ctx:
+        sb = ctx.enter_context(tc.tile_pool(name="sb", bufs=1))
+        ps = ctx.enter_context(tc.psum_pool(name="ps", bufs=1))
+
+        offsets = sb.tile([P, SLOTS // 16], U16, name="offsets")
+        nc.sync.dma_start(offsets[:], offs)
+
+        q_raw = [sb.tile([P, PACK, QUERIES], F32, name=f"q_raw{o}") for o in range(2)]
+        word_pool = sb.tile([P, TOKENS], I32, name="word_pool", align_bytes=64)
+        q_rows = qT[0].rearrange("(o p r) q -> o p r q", o=2, r=PACK)
+        nc.scalar.dma_start(q_raw[0][:], q_rows[0])
+        nc.scalar.dma_start(word_pool[:], k_words[0].rearrange("p t b -> p (t b)").bitcast(I32))
+        nc.scalar.dma_start(q_raw[1][:], q_rows[1])
+
+        scale_pool = sb.tile([P, TOKENS], U8, name="scale_pool", tag="after_scales", align_bytes=64)
+        nc.vector.memset(scale_pool[:].bitcast(I32), 0)
+        scale_rows = k_scales.bitcast(I32).rearrange("o (c r) t -> r c o t", r=4)
+        for r in range(4):
+            nc.sync.dma_start(scale_pool[r:P:SHIFT, :].bitcast(I32), scale_rows[r])
+
+        bias_pool = sb.tile([P, TOKENS], F32, name="bias_pool", tag="after_bias", align_bytes=64)
+        nc.vector.memset(bias_pool[:], 0.0)
+        nc.sync.dma_start(bias_pool[BIAS_ROW : BIAS_ROW + 1, :], kb[0:1, :])
+
+        k_scale1 = sb.tile([P, SLOTS], U8, name="k_scale1", align_bytes=64)
+        nc.vector.memset(k_scale1[:].bitcast(I32), 0)
+
+        ident = sb.tile([P, P], F32, name="ident")
+        make_identity(nc, ident[:])
+
+        warm = sb.tile([P, 1], F32, name="warm")
+        nc.scalar.activation(warm[:], ident[:, 0:1], TANH)
+
+        k_scale0 = sb.tile([P, SLOTS], U8, name="k_scale0", align_bytes=64)
+        nc.vector.tensor_copy(k_scale0[:], scale_pool[:].indirect(offsets[:]))
+        nc.sync.dma_start(k_scale1[0 : P - SHIFT, :].bitcast(I32), k_scale0[SHIFT:P, :].bitcast(I32))
+        k_scale = [k_scale0, k_scale1]
+
+        q_scale = [sb.tile([P, QUERIES], U8, name=f"q_scale{o}", align_bytes=64) for o in range(2)]
+
+        def interleave(grouped, o, cols):
+            src = q_raw[o][:, :, cols].rearrange("p r (c i) -> p c r i", i=4)
+            nc.scalar.copy(grouped[:, cols, :].rearrange("p (c i) r -> p c r i", i=4), src)
+
+        def quantise(codes, grouped, o, cols):
+            nc.vector.quantize_mx(
+                out=codes[:, cols].bitcast(FP8X4),
+                scales=q_scale[o][:, cols],
+                in_=grouped[:, cols, :].rearrange("p q r -> p (q r)"),
+            )
+
+        blocks = [slice(b * P, (b + 1) * P) for b in range(2)]
+        grouped0 = sb.tile([P, QUERIES, PACK], BF16, name="grouped0", align_bytes=64)
+        interleave(grouped0, 0, slice(0, QUERIES))
+        q_codes0 = sb.tile([P, QUERIES], U32, name="q_codes0", tag="after_scales", align_bytes=64)
+        quantise(q_codes0, grouped0, 0, slice(0, QUERIES))
+
+        bias_row = sb.tile([P, SLOTS], F32, name="bias_row", tag="after_turn", align_bytes=64)
+        nc.vector.tensor_copy(bias_row[:], bias_pool[:].indirect(offsets[:]))
+        turned = ps.tile([P, 4, P], F32, name="turned")
+        for j in range(4):
+            nc.tensor.transpose(turned[:, j, :], bias_row[:, j * P : (j + 1) * P], ident[:])
+        bias_cols = sb.tile([P, 4], F32, name="bias_cols")
+        nc.scalar.copy(bias_cols[:], turned[:, :, BIAS_ROW])
+        bias = ps.tile([P, SLOTS], F32, name="bias")
+        for j in range(4):
+            nc.tensor.transpose(bias[:, j * P : (j + 1) * P], bias_cols[:, j : j + 1].to_broadcast([P, P]), ident[:])
+
+        words = sb.tile([P, SLOTS], U32, name="words", tag="after_bias", align_bytes=64)
+        nc.vector.tensor_copy(words[:], word_pool[:].bitcast(U32).indirect(offsets[:]))
+        k_codes = [sb.tile([P, 2 * SLOTS], U8, name=f"k_codes{o}", align_bytes=64) for o in range(2)]
+        halves = words[:].bitcast(U16).rearrange("p (n o) -> p o n", o=2)
+        for o in range(2):
+            nc.vector.tensor_copy(k_codes[o][:].bitcast(U16), halves[:, o, :])
+
+        scores = [ps.tile([P, SLOTS], F32, name=f"scores{b}") for b in range(2)]
+
+        def multiply(codes, o, b):
+            nc.tensor.matmul_mx(
+                out=scores[b][:],
+                lhsT=codes[:, blocks[b]].bitcast(FP8X4),
+                lhsT_scale=q_scale[o][:, blocks[b]],
+                rhs=k_codes[o][:].bitcast(FP4X4),
+                rhs_scale=k_scale[o][:],
+                start=(o == 0),
+                stop=(o == 1),
+            )
+
+        for b in range(2):
+            multiply(q_codes0, 0, b)
+
+        grouped1 = sb.tile([P, QUERIES, PACK], BF16, name="grouped1", tag="after_turn", align_bytes=64)
+        q_codes1 = sb.tile([P, QUERIES], U32, name="q_codes1", tag="after_bias", align_bytes=64)
+        for b in range(2):
+            interleave(grouped1, 1, blocks[b])
+            quantise(q_codes1, grouped1, 1, blocks[b])
+            multiply(q_codes1, 1, b)
+
+        for b in range(2):
+            for c in range(SLOTS // CHUNK):
+                cols = slice(c * CHUNK, (c + 1) * CHUNK)
+                capped = sb.tile([P, CHUNK], F32, name=f"capped{b}{c}")
+                nc.scalar.activation(capped[:], scores[b][:, cols], TANH, scale=1.0 / CAP)
+                result = sb.tile([P, CHUNK], F32, name=f"result{b}{c}")
+                nc.vector.scalar_tensor_tensor(result[:], capped[:], CAP, bias[:, cols], MULT, ADD)
+                nc.sync.dma_start(out[0, b * P : (b + 1) * P, cols], result[:])

@@ -38,58 +38,43 @@ def tile_attend_capkb_kernel(tc, qT, k_words, k_scales, kb, offs, out):
 
         offsets = sb.tile([P, SLOTS // 16], U16, name="offsets")
         nc.sync.dma_start(offsets[:], offs)
-
-        q_raw = [sb.tile([P, PACK, QUERIES], F32, name=f"q_raw{o}") for o in range(2)]
-        word_pool = sb.tile([P, TOKENS], I32, name="word_pool", align_bytes=64)
         q_rows = qT[0].rearrange("(o p r) q -> o p r q", o=2, r=PACK)
-        nc.scalar.dma_start(q_raw[0][:], q_rows[0])
-        nc.scalar.dma_start(word_pool[:], k_words[0].rearrange("p t b -> p (t b)").bitcast(I32))
-        nc.scalar.dma_start(q_raw[1][:], q_rows[1])
+        q_raw0 = sb.tile([P, PACK, QUERIES], F32, name="q_raw0")
+        nc.sync.dma_start(q_raw0[:], q_rows[0])
 
-        scale_pool = sb.tile([P, TOKENS], U8, name="scale_pool", tag="after_scales", align_bytes=64)
+        scale_pool = sb.tile([P, TOKENS], U8, name="scale_pool", align_bytes=64)
         nc.vector.memset(scale_pool[:].bitcast(I32), 0)
         scale_rows = k_scales.bitcast(I32).rearrange("o (c r) t -> r c o t", r=4)
         for r in range(4):
             nc.sync.dma_start(scale_pool[r:P:SHIFT, :].bitcast(I32), scale_rows[r])
-
-        bias_pool = sb.tile([P, TOKENS], F32, name="bias_pool", tag="after_bias", align_bytes=64)
+        bias_pool = sb.tile([P, TOKENS], F32, name="bias_pool", align_bytes=64)
         nc.vector.memset(bias_pool[:], 0.0)
         nc.sync.dma_start(bias_pool[BIAS_ROW : BIAS_ROW + 1, :], kb[0:1, :])
+
+        warm_in = sb.tile([P, 1], F32, name="warm_in", tag="words_slot", align_bytes=64)
+        warm_out = sb.tile([P, 1], F32, name="warm_out", tag="queries_slot", align_bytes=64)
+        nc.vector.memset(warm_in[:], 0.0)
+        nc.scalar.activation(warm_out[:], warm_in[:], TANH)
+
+        word_pool = sb.tile([P, TOKENS], I32, name="word_pool", tag="words_slot", align_bytes=64)
+        nc.sync.dma_start(word_pool[:], k_words[0].rearrange("p t b -> p (t b)").bitcast(I32))
+        q_raw1 = sb.tile([P, PACK, QUERIES], F32, name="q_raw1", tag="queries_slot", align_bytes=64)
+        nc.sync.dma_start(q_raw1[:], q_rows[1])
+        q_raw = [q_raw0, q_raw1]
 
         k_scale1 = sb.tile([P, SLOTS], U8, name="k_scale1", align_bytes=64)
         nc.vector.memset(k_scale1[:].bitcast(I32), 0)
 
         ident = sb.tile([P, P], F32, name="ident")
-        make_identity(nc, ident[:])
-
-        warm = sb.tile([P, 1], F32, name="warm")
-        nc.scalar.activation(warm[:], ident[:, 0:1], TANH)
+        nc.vector.memset(ident[:], 0.0)
+        make_identity(nc, ident[:], nomemset=True)
 
         k_scale0 = sb.tile([P, SLOTS], U8, name="k_scale0", align_bytes=64)
         nc.vector.tensor_copy(k_scale0[:], scale_pool[:].indirect(offsets[:]))
         nc.sync.dma_start(k_scale1[0 : P - SHIFT, :].bitcast(I32), k_scale0[SHIFT:P, :].bitcast(I32))
         k_scale = [k_scale0, k_scale1]
 
-        q_scale = [sb.tile([P, QUERIES], U8, name=f"q_scale{o}", align_bytes=64) for o in range(2)]
-
-        def interleave(grouped, o, cols):
-            src = q_raw[o][:, :, cols].rearrange("p r (c i) -> p c r i", i=4)
-            nc.scalar.copy(grouped[:, cols, :].rearrange("p (c i) r -> p c r i", i=4), src)
-
-        def quantise(codes, grouped, o, cols):
-            nc.vector.quantize_mx(
-                out=codes[:, cols].bitcast(FP8X4),
-                scales=q_scale[o][:, cols],
-                in_=grouped[:, cols, :].rearrange("p q r -> p (q r)"),
-            )
-
-        blocks = [slice(b * P, (b + 1) * P) for b in range(2)]
-        grouped0 = sb.tile([P, QUERIES, PACK], BF16, name="grouped0", align_bytes=64)
-        interleave(grouped0, 0, slice(0, QUERIES))
-        q_codes0 = sb.tile([P, QUERIES], U32, name="q_codes0", tag="after_scales", align_bytes=64)
-        quantise(q_codes0, grouped0, 0, slice(0, QUERIES))
-
-        bias_row = sb.tile([P, SLOTS], F32, name="bias_row", tag="after_turn", align_bytes=64)
+        bias_row = sb.tile([P, SLOTS], F32, name="bias_row", align_bytes=64)
         nc.vector.tensor_copy(bias_row[:], bias_pool[:].indirect(offsets[:]))
         turned = ps.tile([P, 4, P], F32, name="turned")
         for j in range(4):
@@ -100,7 +85,7 @@ def tile_attend_capkb_kernel(tc, qT, k_words, k_scales, kb, offs, out):
         for j in range(4):
             nc.tensor.transpose(bias[:, j * P : (j + 1) * P], bias_cols[:, j : j + 1].to_broadcast([P, P]), ident[:])
 
-        words = sb.tile([P, SLOTS], U32, name="words", tag="after_bias", align_bytes=64)
+        words = sb.tile([P, SLOTS], U32, name="words", align_bytes=64)
         nc.vector.tensor_copy(words[:], word_pool[:].bitcast(U32).indirect(offsets[:]))
         k_codes = [sb.tile([P, 2 * SLOTS], U8, name=f"k_codes{o}", align_bytes=64) for o in range(2)]
         halves = words[:].bitcast(U16).rearrange("p (n o) -> p o n", o=2)
@@ -108,33 +93,45 @@ def tile_attend_capkb_kernel(tc, qT, k_words, k_scales, kb, offs, out):
             nc.vector.tensor_copy(k_codes[o][:].bitcast(U16), halves[:, o, :])
 
         scores = [ps.tile([P, SLOTS], F32, name=f"scores{b}") for b in range(2)]
-
-        def multiply(codes, o, b):
-            nc.tensor.matmul_mx(
-                out=scores[b][:],
-                lhsT=codes[:, blocks[b]].bitcast(FP8X4),
-                lhsT_scale=q_scale[o][:, blocks[b]],
-                rhs=k_codes[o][:].bitcast(FP4X4),
-                rhs_scale=k_scale[o][:],
-                start=(o == 0),
-                stop=(o == 1),
-            )
-
-        for b in range(2):
-            multiply(q_codes0, 0, b)
-
-        grouped1 = sb.tile([P, QUERIES, PACK], BF16, name="grouped1", tag="after_turn", align_bytes=64)
-        q_codes1 = sb.tile([P, QUERIES], U32, name="q_codes1", tag="after_bias", align_bytes=64)
-        for b in range(2):
-            interleave(grouped1, 1, blocks[b])
-            quantise(q_codes1, grouped1, 1, blocks[b])
-            multiply(q_codes1, 1, b)
+        q_codes = {}
+        q_scale = {}
+        for o in range(2):
+            for b in range(2):
+                grouped = sb.tile([P, P, PACK], BF16, name=f"grouped{o}{b}", align_bytes=64)
+                nc.scalar.copy(
+                    grouped[:].rearrange("p (c i) r -> p c r i", i=4),
+                    q_raw[o][:, :, b * P : (b + 1) * P].rearrange("p r (c i) -> p c r i", i=4),
+                )
+                q_codes[o, b] = sb.tile([P, P], U32, name=f"q_codes{o}{b}", align_bytes=64)
+                q_scale[o, b] = sb.tile([P, P], U8, name=f"q_scale{o}{b}", align_bytes=64)
+                nc.vector.quantize_mx(
+                    out=q_codes[o, b][:].bitcast(FP8X4),
+                    scales=q_scale[o, b][:],
+                    in_=grouped[:].rearrange("p q r -> p (q r)"),
+                )
 
         for b in range(2):
+            for o in range(2):
+                nc.tensor.matmul_mx(
+                    out=scores[b][:],
+                    lhsT=q_codes[o, b][:].bitcast(FP8X4),
+                    lhsT_scale=q_scale[o, b][:],
+                    rhs=k_codes[o][:].bitcast(FP4X4),
+                    rhs_scale=k_scale[o][:],
+                    start=(o == 0),
+                    stop=(o == 1),
+                )
+
+        for b in range(2):
+            rows = slice(b * P, (b + 1) * P)
+            result = sb.tile([P, SLOTS], F32, name=f"result{b}")
             for c in range(SLOTS // CHUNK):
                 cols = slice(c * CHUNK, (c + 1) * CHUNK)
                 capped = sb.tile([P, CHUNK], F32, name=f"capped{b}{c}")
                 nc.scalar.activation(capped[:], scores[b][:, cols], TANH, scale=1.0 / CAP)
-                result = sb.tile([P, CHUNK], F32, name=f"result{b}{c}")
-                nc.vector.scalar_tensor_tensor(result[:], capped[:], CAP, bias[:, cols], MULT, ADD)
-                nc.sync.dma_start(out[0, b * P : (b + 1) * P, cols], result[:])
+                nc.vector.scalar_tensor_tensor(result[:, cols], capped[:], CAP, bias[:, cols], MULT, ADD)
+                if b == 1:
+                    queue = nc.sync if c == 0 else nc.scalar
+                    queue.dma_start(out[0, rows, cols], result[:, cols])
+            if b == 0:
+                nc.sync.dma_start(out[0, rows, :], result[:])

@@ -23,7 +23,7 @@ FEATURES = 1024
 QUERIES = 256
 CAP = 30.0
 SHIFT = 16
-BIAS_ROW = 8
+BIAS_ROW = 127
 CHUNK = 256
 
 FLOPS = 2 * FEATURES * QUERIES * SLOTS
@@ -38,41 +38,31 @@ def tile_attend_capkb_kernel(tc, qT, k_words, k_scales, kb, offs, out):
 
         offsets = sb.tile([P, SLOTS // 16], U16, name="offsets")
         nc.sync.dma_start(offsets[:], offs)
+        bias_pool = sb.tile([P, TOKENS], F32, name="bias_pool", align_bytes=64)
+        nc.sync.dma_start(bias_pool[BIAS_ROW : BIAS_ROW + 1, :], kb[0:1, :])
+
         q_rows = qT[0].rearrange("(o p r) q -> o p r q", o=2, r=PACK)
-        q_raw0 = sb.tile([P, PACK, QUERIES], F32, name="q_raw0")
-        nc.sync.dma_start(q_raw0[:], q_rows[0])
+        q_raw = [sb.tile([P, PACK, QUERIES], F32, name=f"q_raw{o}") for o in range(2)]
+        nc.sync.dma_start(q_raw[0][:, 0:2, :], q_rows[0][:, 0:2, :])
 
         scale_pool = sb.tile([P, TOKENS], U8, name="scale_pool", align_bytes=64)
         nc.vector.memset(scale_pool[:].bitcast(I32), 0)
         scale_rows = k_scales.bitcast(I32).rearrange("o (c r) t -> r c o t", r=4)
         for r in range(4):
             nc.sync.dma_start(scale_pool[r:P:SHIFT, :].bitcast(I32), scale_rows[r])
-        bias_pool = sb.tile([P, TOKENS], F32, name="bias_pool", align_bytes=64)
-        nc.vector.memset(bias_pool[:], 0.0)
-        nc.sync.dma_start(bias_pool[BIAS_ROW : BIAS_ROW + 1, :], kb[0:1, :])
+        nc.vector.memset(bias_pool[0:BIAS_ROW, :].bitcast(I32), 0)
 
-        warm_in = sb.tile([P, 1], F32, name="warm_in", tag="words_slot", align_bytes=64)
-        warm_out = sb.tile([P, 1], F32, name="warm_out", tag="queries_slot", align_bytes=64)
-        nc.vector.memset(warm_in[:], 0.0)
-        nc.scalar.activation(warm_out[:], warm_in[:], TANH)
-
-        word_pool = sb.tile([P, TOKENS], I32, name="word_pool", tag="words_slot", align_bytes=64)
+        word_pool = sb.tile([P, TOKENS], I32, name="word_pool", align_bytes=64)
         nc.sync.dma_start(word_pool[:], k_words[0].rearrange("p t b -> p (t b)").bitcast(I32))
-        q_raw1 = sb.tile([P, PACK, QUERIES], F32, name="q_raw1", tag="queries_slot", align_bytes=64)
-        nc.sync.dma_start(q_raw1[:], q_rows[1])
-        q_raw = [q_raw0, q_raw1]
+        nc.sync.dma_start(q_raw[0][:, 2:4, :], q_rows[0][:, 2:4, :])
+        nc.sync.dma_start(q_raw[1][:], q_rows[1])
 
         k_scale1 = sb.tile([P, SLOTS], U8, name="k_scale1", align_bytes=64)
         nc.vector.memset(k_scale1[:].bitcast(I32), 0)
 
         ident = sb.tile([P, P], F32, name="ident")
-        nc.vector.memset(ident[:], 0.0)
+        nc.vector.memset(ident[:].bitcast(I32), 0)
         make_identity(nc, ident[:], nomemset=True)
-
-        k_scale0 = sb.tile([P, SLOTS], U8, name="k_scale0", align_bytes=64)
-        nc.vector.tensor_copy(k_scale0[:], scale_pool[:].indirect(offsets[:]))
-        nc.sync.dma_start(k_scale1[0 : P - SHIFT, :].bitcast(I32), k_scale0[SHIFT:P, :].bitcast(I32))
-        k_scale = [k_scale0, k_scale1]
 
         bias_row = sb.tile([P, SLOTS], F32, name="bias_row", align_bytes=64)
         nc.vector.tensor_copy(bias_row[:], bias_pool[:].indirect(offsets[:]))
@@ -80,58 +70,52 @@ def tile_attend_capkb_kernel(tc, qT, k_words, k_scales, kb, offs, out):
         for j in range(4):
             nc.tensor.transpose(turned[:, j, :], bias_row[:, j * P : (j + 1) * P], ident[:])
         bias_cols = sb.tile([P, 4], F32, name="bias_cols")
-        nc.scalar.copy(bias_cols[:], turned[:, :, BIAS_ROW])
+        nc.scalar.activation(bias_cols[:], turned[:, :, BIAS_ROW], mybir.ActivationFunctionType.Copy)
         bias = ps.tile([P, SLOTS], F32, name="bias")
         for j in range(4):
             nc.tensor.transpose(bias[:, j * P : (j + 1) * P], bias_cols[:, j : j + 1].to_broadcast([P, P]), ident[:])
 
+        k_scale0 = sb.tile([P, SLOTS], U8, name="k_scale0", align_bytes=64)
+        nc.vector.tensor_copy(k_scale0[:], scale_pool[:].indirect(offsets[:]))
+        nc.sync.dma_start(k_scale1[0 : P - SHIFT, :].bitcast(I32), k_scale0[SHIFT:P, :].bitcast(I32))
+        k_scale = [k_scale0, k_scale1]
+
         words = sb.tile([P, SLOTS], U32, name="words", align_bytes=64)
         nc.vector.tensor_copy(words[:], word_pool[:].bitcast(U32).indirect(offsets[:]))
-        k_codes = [sb.tile([P, 2 * SLOTS], U8, name=f"k_codes{o}", align_bytes=64) for o in range(2)]
         halves = words[:].bitcast(U16).rearrange("p (n o) -> p o n", o=2)
-        for o in range(2):
-            nc.vector.tensor_copy(k_codes[o][:].bitcast(U16), halves[:, o, :])
 
         scores = [ps.tile([P, SLOTS], F32, name=f"scores{b}") for b in range(2)]
-        q_codes = {}
-        q_scale = {}
         for o in range(2):
+            k_codes = sb.tile([P, 2 * SLOTS], U8, name=f"k_codes{o}", tag=f"slot{o}", align_bytes=64)
+            nc.vector.tensor_copy(k_codes[:].bitcast(U16), halves[:, o, :])
             for b in range(2):
-                grouped = sb.tile([P, P, PACK], BF16, name=f"grouped{o}{b}", align_bytes=64)
-                nc.scalar.copy(
+                grouped = sb.tile([P, P, PACK], BF16, name=f"grouped{o}{b}", tag=f"slot{1 + 2 * o + b}", align_bytes=64)
+                copy = nc.vector.tensor_copy if (o, b) == (1, 1) else nc.scalar.copy
+                copy(
                     grouped[:].rearrange("p (c i) r -> p c r i", i=4),
                     q_raw[o][:, :, b * P : (b + 1) * P].rearrange("p r (c i) -> p c r i", i=4),
                 )
-                q_codes[o, b] = sb.tile([P, P], U32, name=f"q_codes{o}{b}", align_bytes=64)
-                q_scale[o, b] = sb.tile([P, P], U8, name=f"q_scale{o}{b}", align_bytes=64)
+                q_codes = sb.tile([P, P], U32, name=f"q_codes{o}{b}", align_bytes=64)
+                q_scale = sb.tile([P, P], U8, name=f"q_scale{o}{b}", align_bytes=64)
                 nc.vector.quantize_mx(
-                    out=q_codes[o, b][:].bitcast(FP8X4),
-                    scales=q_scale[o, b][:],
-                    in_=grouped[:].rearrange("p q r -> p (q r)"),
+                    out=q_codes[:].bitcast(FP8X4), scales=q_scale[:], in_=grouped[:].rearrange("p q r -> p (q r)")
                 )
-
-        for b in range(2):
-            for o in range(2):
                 nc.tensor.matmul_mx(
                     out=scores[b][:],
-                    lhsT=q_codes[o, b][:].bitcast(FP8X4),
-                    lhsT_scale=q_scale[o, b][:],
-                    rhs=k_codes[o][:].bitcast(FP4X4),
+                    lhsT=q_codes[:].bitcast(FP8X4),
+                    lhsT_scale=q_scale[:],
+                    rhs=k_codes[:].bitcast(FP4X4),
                     rhs_scale=k_scale[o][:],
                     start=(o == 0),
                     stop=(o == 1),
                 )
 
-        for b in range(2):
-            rows = slice(b * P, (b + 1) * P)
-            result = sb.tile([P, SLOTS], F32, name=f"result{b}")
-            for c in range(SLOTS // CHUNK):
-                cols = slice(c * CHUNK, (c + 1) * CHUNK)
-                capped = sb.tile([P, CHUNK], F32, name=f"capped{b}{c}")
+        for b, cuts in enumerate(((0, 256, 512), (0, 256, 512))):
+            for c in range(2):
+                cols = slice(cuts[c], cuts[c + 1])
+                width = cuts[c + 1] - cuts[c]
+                capped = sb.tile([P, width], F32, name=f"capped{b}{c}")
                 nc.scalar.activation(capped[:], scores[b][:, cols], TANH, scale=1.0 / CAP)
-                nc.vector.scalar_tensor_tensor(result[:, cols], capped[:], CAP, bias[:, cols], MULT, ADD)
-                if b == 1:
-                    queue = nc.sync if c == 0 else nc.scalar
-                    queue.dma_start(out[0, rows, cols], result[:, cols])
-            if b == 0:
-                nc.sync.dma_start(out[0, rows, :], result[:])
+                result = sb.tile([P, width], F32, name=f"result{b}{c}")
+                nc.vector.scalar_tensor_tensor(result[:], capped[:], CAP, bias[:, cols], MULT, ADD)
+                nc.sync.dma_start(out[0, b * P : (b + 1) * P, cols], result[:])

@@ -25,6 +25,8 @@ CAP = 30.0
 SHIFT = 16
 BIAS_ROW = 127
 CHUNK = 256
+EARLY = 768
+VECTOR_ZEROS = 1536
 
 FLOPS = 2 * FEATURES * QUERIES * SLOTS
 BYTES = 4 * FEATURES * QUERIES + 4 * P * TOKENS + 32 * TOKENS + 4 * TOKENS + 2 * P * SLOTS // 16 + 4 * QUERIES * SLOTS
@@ -43,25 +45,27 @@ def tile_attend_capkb_kernel(tc, qT, k_words, k_scales, kb, offs, out):
 
         q_rows = qT[0].rearrange("(o p r) q -> o p r q", o=2, r=PACK)
         q_raw = [sb.tile([P, PACK, QUERIES], F32, name=f"q_raw{o}") for o in range(2)]
-        nc.sync.dma_start(q_raw[0][:, 0:2, :], q_rows[0][:, 0:2, :])
+        word_pool = sb.tile([P, TOKENS], I32, name="word_pool", align_bytes=64)
+        pool_rows = k_words[0].rearrange("p t b -> p (t b)").bitcast(I32)
+        nc.sync.dma_start(word_pool[:, 0:EARLY], pool_rows[:, 0:EARLY])
 
         scale_pool = sb.tile([P, TOKENS], U8, name="scale_pool", align_bytes=64)
-        nc.vector.memset(scale_pool[:].bitcast(I32), 0)
+        nc.gpsimd.memset(scale_pool[:].bitcast(I32), 0)
         scale_rows = k_scales.bitcast(I32).rearrange("o (c r) t -> r c o t", r=4)
         for r in range(4):
             nc.sync.dma_start(scale_pool[r:P:SHIFT, :].bitcast(I32), scale_rows[r])
-        nc.vector.memset(bias_pool[0:BIAS_ROW, :].bitcast(I32), 0)
 
-        word_pool = sb.tile([P, TOKENS], I32, name="word_pool", align_bytes=64)
-        nc.sync.dma_start(word_pool[:], k_words[0].rearrange("p t b -> p (t b)").bitcast(I32))
-        nc.sync.dma_start(q_raw[0][:, 2:4, :], q_rows[0][:, 2:4, :])
-        nc.sync.dma_start(q_raw[1][:], q_rows[1])
+        nc.sync.dma_start(word_pool[:, EARLY:TOKENS], pool_rows[:, EARLY:TOKENS])
+        for o in range(2):
+            nc.sync.dma_start(q_raw[o][:], q_rows[o])
 
         k_scale1 = sb.tile([P, SLOTS], U8, name="k_scale1", align_bytes=64)
         nc.vector.memset(k_scale1[:].bitcast(I32), 0)
 
         ident = sb.tile([P, P], F32, name="ident")
         nc.vector.memset(ident[:].bitcast(I32), 0)
+        nc.vector.memset(bias_pool[0:BIAS_ROW, 0:VECTOR_ZEROS].bitcast(I32), 0)
+        nc.gpsimd.memset(bias_pool[0:BIAS_ROW, VECTOR_ZEROS:TOKENS].bitcast(I32), 0)
         make_identity(nc, ident[:], nomemset=True)
 
         bias_row = sb.tile([P, SLOTS], F32, name="bias_row", align_bytes=64)
@@ -90,7 +94,7 @@ def tile_attend_capkb_kernel(tc, qT, k_words, k_scales, kb, offs, out):
             nc.vector.tensor_copy(k_codes[:].bitcast(U16), halves[:, o, :])
             for b in range(2):
                 grouped = sb.tile([P, P, PACK], BF16, name=f"grouped{o}{b}", tag=f"slot{1 + 2 * o + b}", align_bytes=64)
-                copy = nc.vector.tensor_copy if (o, b) == (1, 1) else nc.scalar.copy
+                copy = nc.vector.tensor_copy if (o, b) == (1, 0) else nc.scalar.copy
                 copy(
                     grouped[:].rearrange("p (c i) r -> p c r i", i=4),
                     q_raw[o][:, :, b * P : (b + 1) * P].rearrange("p r (c i) -> p c r i", i=4),

@@ -12,21 +12,25 @@ U8 = mybir.dt.uint8
 FP8X4 = mybir.dt.float8_e4m3fn_x4
 FP4X4 = mybir.dt.float4_e2m1fn_x4
 TANH = mybir.ActivationFunctionType.Tanh
+COPY = mybir.ActivationFunctionType.Copy
 MULT = mybir.AluOpType.mult
 ADD = mybir.AluOpType.add
 
 P = 128
 PACK = 4
+PASSES = 2
+BLOCKS = 2
 SLOTS = 512
 TOKENS = 2048
-FEATURES = 1024
-QUERIES = 256
+FEATURES = PASSES * PACK * P
+QUERIES = BLOCKS * P
 CAP = 30.0
+SCALE_ROWS = 4
 SHIFT = 16
-BIAS_ROW = 127
+BIAS_ROW = P - 1
+LINE = 4
 CHUNK = 256
-EARLY = 768
-VECTOR_ZEROS = 1536
+EARLY_TOKENS = 512
 
 FLOPS = 2 * FEATURES * QUERIES * SLOTS
 BYTES = 4 * FEATURES * QUERIES + 4 * P * TOKENS + 32 * TOKENS + 4 * TOKENS + 2 * P * SLOTS // 16 + 4 * QUERIES * SLOTS
@@ -41,42 +45,42 @@ def tile_attend_capkb_kernel(tc, qT, k_words, k_scales, kb, offs, out):
         offsets = sb.tile([P, SLOTS // 16], U16, name="offsets")
         nc.sync.dma_start(offsets[:], offs)
         bias_pool = sb.tile([P, TOKENS], F32, name="bias_pool", align_bytes=64)
-        nc.sync.dma_start(bias_pool[BIAS_ROW : BIAS_ROW + 1, :], kb[0:1, :])
+        nc.sync.dma_start(bias_pool[BIAS_ROW:P, :], kb[0:1, :])
 
-        q_rows = qT[0].rearrange("(o p r) q -> o p r q", o=2, r=PACK)
-        q_raw = [sb.tile([P, PACK, QUERIES], F32, name=f"q_raw{o}") for o in range(2)]
+        q_rows = qT[0].rearrange("(o p r) q -> o p r q", o=PASSES, r=PACK)
+        q_raw = [sb.tile([P, PACK, QUERIES], F32, name=f"q_raw{o}") for o in range(PASSES)]
         word_pool = sb.tile([P, TOKENS], I32, name="word_pool", align_bytes=64)
-        pool_rows = k_words[0].rearrange("p t b -> p (t b)").bitcast(I32)
-        nc.sync.dma_start(word_pool[:, 0:EARLY], pool_rows[:, 0:EARLY])
+        word_rows = k_words[0].rearrange("p t b -> p (t b)").bitcast(I32)
+        nc.sync.dma_start(word_pool[:, 0:EARLY_TOKENS], word_rows[:, 0:EARLY_TOKENS])
 
         scale_pool = sb.tile([P, TOKENS], U8, name="scale_pool", align_bytes=64)
         nc.gpsimd.memset(scale_pool[:].bitcast(I32), 0)
-        scale_rows = k_scales.bitcast(I32).rearrange("o (c r) t -> r c o t", r=4)
-        for r in range(4):
+        scale_rows = k_scales.bitcast(I32).rearrange("o (c r) t -> r c o t", r=SCALE_ROWS)
+        for r in range(SCALE_ROWS):
             nc.sync.dma_start(scale_pool[r:P:SHIFT, :].bitcast(I32), scale_rows[r])
 
-        nc.sync.dma_start(word_pool[:, EARLY:TOKENS], pool_rows[:, EARLY:TOKENS])
-        for o in range(2):
+        nc.sync.dma_start(word_pool[:, EARLY_TOKENS:TOKENS], word_rows[:, EARLY_TOKENS:TOKENS])
+        for o in range(PASSES):
             nc.sync.dma_start(q_raw[o][:], q_rows[o])
 
         k_scale1 = sb.tile([P, SLOTS], U8, name="k_scale1", align_bytes=64)
         nc.vector.memset(k_scale1[:].bitcast(I32), 0)
 
         ident = sb.tile([P, P], F32, name="ident")
+        nc.vector.memset(bias_pool[0:BIAS_ROW, :].bitcast(I32), 0)
         nc.vector.memset(ident[:].bitcast(I32), 0)
-        nc.vector.memset(bias_pool[0:BIAS_ROW, 0:VECTOR_ZEROS].bitcast(I32), 0)
-        nc.gpsimd.memset(bias_pool[0:BIAS_ROW, VECTOR_ZEROS:TOKENS].bitcast(I32), 0)
         make_identity(nc, ident[:], nomemset=True)
 
         bias_row = sb.tile([P, SLOTS], F32, name="bias_row", align_bytes=64)
         nc.vector.tensor_copy(bias_row[:], bias_pool[:].indirect(offsets[:]))
-        turned = ps.tile([P, 4, P], F32, name="turned")
-        for j in range(4):
+        slot_tiles = SLOTS // P
+        turned = ps.tile([P, slot_tiles, P], F32, name="turned")
+        for j in range(slot_tiles):
             nc.tensor.transpose(turned[:, j, :], bias_row[:, j * P : (j + 1) * P], ident[:])
-        bias_cols = sb.tile([P, 4], F32, name="bias_cols")
-        nc.scalar.activation(bias_cols[:], turned[:, :, BIAS_ROW], mybir.ActivationFunctionType.Copy)
+        bias_cols = sb.tile([P, slot_tiles], F32, name="bias_cols")
+        nc.scalar.activation(bias_cols[:], turned[:, :, BIAS_ROW], COPY)
         bias = ps.tile([P, SLOTS], F32, name="bias")
-        for j in range(4):
+        for j in range(slot_tiles):
             nc.tensor.transpose(bias[:, j * P : (j + 1) * P], bias_cols[:, j : j + 1].to_broadcast([P, P]), ident[:])
 
         k_scale0 = sb.tile([P, SLOTS], U8, name="k_scale0", align_bytes=64)
@@ -86,18 +90,20 @@ def tile_attend_capkb_kernel(tc, qT, k_words, k_scales, kb, offs, out):
 
         words = sb.tile([P, SLOTS], U32, name="words", align_bytes=64)
         nc.vector.tensor_copy(words[:], word_pool[:].bitcast(U32).indirect(offsets[:]))
-        halves = words[:].bitcast(U16).rearrange("p (n o) -> p o n", o=2)
+        halves = words[:].bitcast(U16).rearrange("p (n o) -> p o n", o=PASSES)
 
-        scores = [ps.tile([P, SLOTS], F32, name=f"scores{b}") for b in range(2)]
-        for o in range(2):
+        scores = [ps.tile([P, SLOTS], F32, name=f"scores{b}") for b in range(BLOCKS)]
+        for o in range(PASSES):
             k_codes = sb.tile([P, 2 * SLOTS], U8, name=f"k_codes{o}", tag=f"slot{o}", align_bytes=64)
             nc.vector.tensor_copy(k_codes[:].bitcast(U16), halves[:, o, :])
-            for b in range(2):
-                grouped = sb.tile([P, P, PACK], BF16, name=f"grouped{o}{b}", tag=f"slot{1 + 2 * o + b}", align_bytes=64)
-                copy = nc.vector.tensor_copy if (o, b) == (1, 0) else nc.scalar.copy
+            for b in range(BLOCKS):
+                grouped = sb.tile(
+                    [P, P, PACK], BF16, name=f"grouped{o}{b}", tag=f"slot{1 + BLOCKS * o + b}", align_bytes=64
+                )
+                copy = nc.vector.tensor_copy if (o, b) == (PASSES - 1, 0) else nc.scalar.copy
                 copy(
-                    grouped[:].rearrange("p (c i) r -> p c r i", i=4),
-                    q_raw[o][:, :, b * P : (b + 1) * P].rearrange("p r (c i) -> p c r i", i=4),
+                    grouped[:].rearrange("p (c i) r -> p c r i", i=LINE),
+                    q_raw[o][:, :, b * P : (b + 1) * P].rearrange("p r (c i) -> p c r i", i=LINE),
                 )
                 q_codes = sb.tile([P, P], U32, name=f"q_codes{o}{b}", align_bytes=64)
                 q_scale = sb.tile([P, P], U8, name=f"q_scale{o}{b}", align_bytes=64)
@@ -111,15 +117,14 @@ def tile_attend_capkb_kernel(tc, qT, k_words, k_scales, kb, offs, out):
                     rhs=k_codes[:].bitcast(FP4X4),
                     rhs_scale=k_scale[o][:],
                     start=(o == 0),
-                    stop=(o == 1),
+                    stop=(o == PASSES - 1),
                 )
 
-        for b, cuts in enumerate(((0, 256, 512), (0, 256, 512))):
-            for c in range(2):
-                cols = slice(cuts[c], cuts[c + 1])
-                width = cuts[c + 1] - cuts[c]
-                capped = sb.tile([P, width], F32, name=f"capped{b}{c}")
+        for b in range(BLOCKS):
+            for c in range(SLOTS // CHUNK):
+                cols = slice(c * CHUNK, (c + 1) * CHUNK)
+                capped = sb.tile([P, CHUNK], F32, name=f"capped{b}{c}")
                 nc.scalar.activation(capped[:], scores[b][:, cols], TANH, scale=1.0 / CAP)
-                result = sb.tile([P, width], F32, name=f"result{b}{c}")
+                result = sb.tile([P, CHUNK], F32, name=f"result{b}{c}")
                 nc.vector.scalar_tensor_tensor(result[:], capped[:], CAP, bias[:, cols], MULT, ADD)
                 nc.sync.dma_start(out[0, b * P : (b + 1) * P, cols], result[:])

@@ -31,6 +31,8 @@ BIAS_ROW = P - 1
 LINE = 4
 CHUNK = 256
 EARLY_TOKENS = 512
+VECTOR_ZEROES = 1664
+STEPS = (((0, 128), (128, 256), (256, 512)), ((0, 256), (256, 384), (384, 512)))
 
 FLOPS = 2 * FEATURES * QUERIES * SLOTS
 BYTES = 4 * FEATURES * QUERIES + 4 * P * TOKENS + 32 * TOKENS + 4 * TOKENS + 2 * P * SLOTS // 16 + 4 * QUERIES * SLOTS
@@ -42,10 +44,10 @@ def tile_attend_capkb_kernel(tc, qT, k_words, k_scales, kb, offs, out):
         sb = ctx.enter_context(tc.tile_pool(name="sb", bufs=1))
         ps = ctx.enter_context(tc.psum_pool(name="ps", bufs=1))
 
-        offsets = sb.tile([P, SLOTS // 16], U16, name="offsets")
-        nc.sync.dma_start(offsets[:], offs)
         bias_pool = sb.tile([P, TOKENS], F32, name="bias_pool", align_bytes=64)
         nc.sync.dma_start(bias_pool[BIAS_ROW:P, :], kb[0:1, :])
+        offsets = sb.tile([P, SLOTS // 16], U16, name="offsets")
+        nc.sync.dma_start(offsets[:], offs)
 
         q_rows = qT[0].rearrange("(o p r) q -> o p r q", o=PASSES, r=PACK)
         q_raw = [sb.tile([P, PACK, QUERIES], F32, name=f"q_raw{o}") for o in range(PASSES)]
@@ -64,12 +66,11 @@ def tile_attend_capkb_kernel(tc, qT, k_words, k_scales, kb, offs, out):
             nc.sync.dma_start(q_raw[o][:], q_rows[o])
 
         k_scale1 = sb.tile([P, SLOTS], U8, name="k_scale1", align_bytes=64)
-        nc.vector.memset(k_scale1[:].bitcast(I32), 0)
-
         ident = sb.tile([P, P], F32, name="ident")
-        nc.vector.memset(bias_pool[0:BIAS_ROW, :].bitcast(I32), 0)
-        nc.vector.memset(ident[:].bitcast(I32), 0)
-        make_identity(nc, ident[:], nomemset=True)
+        nc.vector.memset(bias_pool[0:BIAS_ROW, 0:VECTOR_ZEROES].bitcast(I32), 0)
+        nc.gpsimd.memset(bias_pool[0:BIAS_ROW, VECTOR_ZEROES:TOKENS].bitcast(I32), 0)
+        make_identity(nc, ident[:])
+        nc.gpsimd.memset(k_scale1[:].bitcast(I32), 0)
 
         bias_row = sb.tile([P, SLOTS], F32, name="bias_row", align_bytes=64)
         nc.vector.tensor_copy(bias_row[:], bias_pool[:].indirect(offsets[:]))
@@ -92,16 +93,18 @@ def tile_attend_capkb_kernel(tc, qT, k_words, k_scales, kb, offs, out):
         nc.vector.tensor_copy(words[:], word_pool[:].bitcast(U32).indirect(offsets[:]))
         halves = words[:].bitcast(U16).rearrange("p (n o) -> p o n", o=PASSES)
 
-        scores = [ps.tile([P, SLOTS], F32, name=f"scores{b}") for b in range(BLOCKS)]
+        scores = [
+            [ps.tile([P, stop - start], F32, name=f"scores{b}{start}") for start, stop in STEPS[b]]
+            for b in range(BLOCKS)
+        ]
         for o in range(PASSES):
-            k_codes = sb.tile([P, 2 * SLOTS], U8, name=f"k_codes{o}", tag=f"slot{o}", align_bytes=64)
+            k_codes = sb.tile([P, 2 * SLOTS], U8, name=f"k_codes{o}", tag=f"slot{2 * o}", align_bytes=64)
             nc.vector.tensor_copy(k_codes[:].bitcast(U16), halves[:, o, :])
             for b in range(BLOCKS):
                 grouped = sb.tile(
                     [P, P, PACK], BF16, name=f"grouped{o}{b}", tag=f"slot{1 + BLOCKS * o + b}", align_bytes=64
                 )
-                copy = nc.vector.tensor_copy if (o, b) == (PASSES - 1, 0) else nc.scalar.copy
-                copy(
+                nc.scalar.copy(
                     grouped[:].rearrange("p (c i) r -> p c r i", i=LINE),
                     q_raw[o][:, :, b * P : (b + 1) * P].rearrange("p r (c i) -> p c r i", i=LINE),
                 )
@@ -110,21 +113,26 @@ def tile_attend_capkb_kernel(tc, qT, k_words, k_scales, kb, offs, out):
                 nc.vector.quantize_mx(
                     out=q_codes[:].bitcast(FP8X4), scales=q_scale[:], in_=grouped[:].rearrange("p q r -> p (q r)")
                 )
-                nc.tensor.matmul_mx(
-                    out=scores[b][:],
-                    lhsT=q_codes[:].bitcast(FP8X4),
-                    lhsT_scale=q_scale[:],
-                    rhs=k_codes[:].bitcast(FP4X4),
-                    rhs_scale=k_scale[o][:],
-                    start=(o == 0),
-                    stop=(o == PASSES - 1),
-                )
+                for bank, (start, stop) in zip(scores[b], STEPS[b]):
+                    for n in range(start, stop, P):
+                        nc.tensor.matmul_mx(
+                            out=bank[:, n - start : n - start + P],
+                            lhsT=q_codes[:].bitcast(FP8X4),
+                            lhsT_scale=q_scale[:],
+                            rhs=k_codes[:, 2 * n : 2 * (n + P)].bitcast(FP4X4),
+                            rhs_scale=k_scale[o][:, n : n + P],
+                            start=(o == 0 and n == start),
+                            stop=(o == PASSES - 1 and n + P == stop),
+                        )
 
         for b in range(BLOCKS):
-            for c in range(SLOTS // CHUNK):
-                cols = slice(c * CHUNK, (c + 1) * CHUNK)
-                capped = sb.tile([P, CHUNK], F32, name=f"capped{b}{c}")
-                nc.scalar.activation(capped[:], scores[b][:, cols], TANH, scale=1.0 / CAP)
-                result = sb.tile([P, CHUNK], F32, name=f"result{b}{c}")
-                nc.vector.scalar_tensor_tensor(result[:], capped[:], CAP, bias[:, cols], MULT, ADD)
-                nc.sync.dma_start(out[0, b * P : (b + 1) * P, cols], result[:])
+            results = [sb.tile([P, CHUNK], F32, name=f"result{b}{c}") for c in range(SLOTS // CHUNK)]
+            for bank, (start, stop) in zip(scores[b], STEPS[b]):
+                c = start // CHUNK
+                capped = sb.tile([P, stop - start], F32, name=f"capped{b}{start}")
+                nc.scalar.activation(capped[:], bank[:], TANH, scale=1.0 / CAP)
+                nc.vector.scalar_tensor_tensor(
+                    results[c][:, start - c * CHUNK : stop - c * CHUNK], capped[:], CAP, bias[:, start:stop], MULT, ADD
+                )
+                if stop % CHUNK == 0:
+                    nc.sync.dma_start(out[0, b * P : (b + 1) * P, c * CHUNK : (c + 1) * CHUNK], results[c][:])

@@ -29,10 +29,11 @@ SCALE_ROWS = 4
 SHIFT = 16
 BIAS_ROW = P - 1
 LINE = 4
-CHUNK = 256
+HALF = SLOTS // 2
 EARLY_TOKENS = 512
 VECTOR_ZEROES = 1664
-STEPS = (((0, 128), (128, 256), (256, 512)), ((0, 256), (256, 384), (384, 512)))
+STEPS = (((0, 128), (128, 256), (256, 512)), ((0, 128), (128, 256), (256, 384), (384, 512)))
+STORES = (((0, 256), (256, 512)), ((0, 384), (384, 512)))
 
 FLOPS = 2 * FEATURES * QUERIES * SLOTS
 BYTES = 4 * FEATURES * QUERIES + 4 * P * TOKENS + 32 * TOKENS + 4 * TOKENS + 2 * P * SLOTS // 16 + 4 * QUERIES * SLOTS
@@ -44,13 +45,14 @@ def tile_attend_capkb_kernel(tc, qT, k_words, k_scales, kb, offs, out):
         sb = ctx.enter_context(tc.tile_pool(name="sb", bufs=1))
         ps = ctx.enter_context(tc.psum_pool(name="ps", bufs=1))
 
+        offsets = sb.tile([P, SLOTS // 16], U16, name="offsets")
         bias_pool = sb.tile([P, TOKENS], F32, name="bias_pool", align_bytes=64)
         nc.sync.dma_start(bias_pool[BIAS_ROW:P, :], kb[0:1, :])
-        offsets = sb.tile([P, SLOTS // 16], U16, name="offsets")
         nc.sync.dma_start(offsets[:], offs)
 
         q_rows = qT[0].rearrange("(o p r) q -> o p r q", o=PASSES, r=PACK)
-        q_raw = [sb.tile([P, PACK, QUERIES], F32, name=f"q_raw{o}") for o in range(PASSES)]
+        q_raw0 = sb.tile([P, PACK, QUERIES], F32, name="q_raw0")
+        q_raw1 = [sb.tile([P, PACK, P], F32, name=f"q_raw1{b}", align_bytes=64) for b in range(BLOCKS)]
         word_pool = sb.tile([P, TOKENS], I32, name="word_pool", align_bytes=64)
         word_rows = k_words[0].rearrange("p t b -> p (t b)").bitcast(I32)
         nc.sync.dma_start(word_pool[:, 0:EARLY_TOKENS], word_rows[:, 0:EARLY_TOKENS])
@@ -62,8 +64,9 @@ def tile_attend_capkb_kernel(tc, qT, k_words, k_scales, kb, offs, out):
             nc.sync.dma_start(scale_pool[r:P:SHIFT, :].bitcast(I32), scale_rows[r])
 
         nc.sync.dma_start(word_pool[:, EARLY_TOKENS:TOKENS], word_rows[:, EARLY_TOKENS:TOKENS])
-        for o in range(PASSES):
-            nc.sync.dma_start(q_raw[o][:], q_rows[o])
+        nc.sync.dma_start(q_raw0[:], q_rows[0])
+        for b in range(BLOCKS):
+            nc.sync.dma_start(q_raw1[b][:], q_rows[1][:, :, b * P : (b + 1) * P])
 
         k_scale1 = sb.tile([P, SLOTS], U8, name="k_scale1", align_bytes=64)
         ident = sb.tile([P, P], F32, name="ident")
@@ -75,7 +78,7 @@ def tile_attend_capkb_kernel(tc, qT, k_words, k_scales, kb, offs, out):
         bias_row = sb.tile([P, SLOTS], F32, name="bias_row", align_bytes=64)
         nc.vector.tensor_copy(bias_row[:], bias_pool[:].indirect(offsets[:]))
         slot_tiles = SLOTS // P
-        turned = ps.tile([P, slot_tiles, P], F32, name="turned")
+        turned = ps.tile([P, slot_tiles, P], F32, name="turned", tag="scores1384")
         for j in range(slot_tiles):
             nc.tensor.transpose(turned[:, j, :], bias_row[:, j * P : (j + 1) * P], ident[:])
         bias_cols = sb.tile([P, slot_tiles], F32, name="bias_cols")
@@ -97,42 +100,66 @@ def tile_attend_capkb_kernel(tc, qT, k_words, k_scales, kb, offs, out):
             [ps.tile([P, stop - start], F32, name=f"scores{b}{start}") for start, stop in STEPS[b]]
             for b in range(BLOCKS)
         ]
-        for o in range(PASSES):
-            k_codes = sb.tile([P, 2 * SLOTS], U8, name=f"k_codes{o}", tag=f"slot{2 * o}", align_bytes=64)
-            nc.vector.tensor_copy(k_codes[:].bitcast(U16), halves[:, o, :])
-            for b in range(BLOCKS):
-                grouped = sb.tile(
-                    [P, P, PACK], BF16, name=f"grouped{o}{b}", tag=f"slot{1 + BLOCKS * o + b}", align_bytes=64
+
+        def part(o, first, last, tag):
+            codes = sb.tile([P, 2 * (last - first)], U8, name=f"k_codes{o}{first}", tag=tag, align_bytes=64)
+            nc.vector.tensor_copy(codes[:].bitcast(U16), halves[:, o, first:last])
+            return [codes[:, 2 * n : 2 * (n + P)] for n in range(0, last - first, P)]
+
+        def interleave(name, raw, copy, tag):
+            grouped = sb.tile([P, P, PACK], BF16, name=name, tag=tag, align_bytes=64)
+            copy(
+                grouped[:].rearrange("p (c i) r -> p c r i", i=LINE),
+                raw.rearrange("p r (c i) -> p c r i", i=LINE),
+            )
+            return grouped
+
+        def quantize(name, grouped):
+            q_codes = sb.tile([P, P], U32, name=f"q_codes{name}", align_bytes=64)
+            q_scale = sb.tile([P, P], U8, name=f"q_scale{name}", align_bytes=64)
+            nc.vector.quantize_mx(
+                out=q_codes[:].bitcast(FP8X4), scales=q_scale[:], in_=grouped[:].rearrange("p q r -> p (q r)")
+            )
+            return q_codes, q_scale
+
+        def multiply(o, b, step, quantized, k_codes):
+            q_codes, q_scale = quantized
+            start, stop = STEPS[b][step]
+            for n in range(start, stop, P):
+                nc.tensor.matmul_mx(
+                    out=scores[b][step][:, n - start : n - start + P],
+                    lhsT=q_codes[:].bitcast(FP8X4),
+                    lhsT_scale=q_scale[:],
+                    rhs=k_codes[n // P].bitcast(FP4X4),
+                    rhs_scale=k_scale[o][:, n : n + P],
+                    start=(o == 0 and n == start),
+                    stop=(o == PASSES - 1 and n + P == stop),
                 )
-                nc.scalar.copy(
-                    grouped[:].rearrange("p (c i) r -> p c r i", i=LINE),
-                    q_raw[o][:, :, b * P : (b + 1) * P].rearrange("p r (c i) -> p c r i", i=LINE),
-                )
-                q_codes = sb.tile([P, P], U32, name=f"q_codes{o}{b}", align_bytes=64)
-                q_scale = sb.tile([P, P], U8, name=f"q_scale{o}{b}", align_bytes=64)
-                nc.vector.quantize_mx(
-                    out=q_codes[:].bitcast(FP8X4), scales=q_scale[:], in_=grouped[:].rearrange("p q r -> p (q r)")
-                )
-                for bank, (start, stop) in zip(scores[b], STEPS[b]):
-                    for n in range(start, stop, P):
-                        nc.tensor.matmul_mx(
-                            out=bank[:, n - start : n - start + P],
-                            lhsT=q_codes[:].bitcast(FP8X4),
-                            lhsT_scale=q_scale[:],
-                            rhs=k_codes[:, 2 * n : 2 * (n + P)].bitcast(FP4X4),
-                            rhs_scale=k_scale[o][:, n : n + P],
-                            start=(o == 0 and n == start),
-                            stop=(o == PASSES - 1 and n + P == stop),
-                        )
+
+        k_codes0 = part(0, 0, SLOTS, "k_codes0")
+        q00 = quantize("00", interleave("grouped00", q_raw0[:, :, 0:P], nc.scalar.copy, "grouped00"))
+        for step in range(len(STEPS[0])):
+            multiply(0, 0, step, q00, k_codes0)
+        k_codes1 = part(1, 0, SLOTS, "grouped00")
+        q10 = quantize("10", interleave("grouped10", q_raw1[0][:], nc.scalar.copy, "grouped10"))
+        for step in range(len(STEPS[0])):
+            multiply(1, 0, step, q10, k_codes1)
+        grouped11 = interleave("grouped11", q_raw1[1][:], nc.vector.tensor_copy, "q_raw10")
+        q01 = quantize("01", interleave("grouped01", q_raw0[:, :, P:QUERIES], nc.scalar.copy, "grouped01"))
+        q11 = quantize("11", grouped11)
+        for step in range(len(STEPS[1])):
+            multiply(0, 1, step, q01, k_codes0)
+            multiply(1, 1, step, q11, k_codes1)
 
         for b in range(BLOCKS):
-            results = [sb.tile([P, CHUNK], F32, name=f"result{b}{c}") for c in range(SLOTS // CHUNK)]
+            results = [sb.tile([P, last - first], F32, name=f"result{b}{first}") for first, last in STORES[b]]
             for bank, (start, stop) in zip(scores[b], STEPS[b]):
-                c = start // CHUNK
                 capped = sb.tile([P, stop - start], F32, name=f"capped{b}{start}")
                 nc.scalar.activation(capped[:], bank[:], TANH, scale=1.0 / CAP)
-                nc.vector.scalar_tensor_tensor(
-                    results[c][:, start - c * CHUNK : stop - c * CHUNK], capped[:], CAP, bias[:, start:stop], MULT, ADD
-                )
-                if stop % CHUNK == 0:
-                    nc.sync.dma_start(out[0, b * P : (b + 1) * P, c * CHUNK : (c + 1) * CHUNK], results[c][:])
+                for result, (first, last) in zip(results, STORES[b]):
+                    if first <= start < last:
+                        nc.vector.scalar_tensor_tensor(
+                            result[:, start - first : stop - first], capped[:], CAP, bias[:, start:stop], MULT, ADD
+                        )
+                        if stop == last:
+                            nc.sync.dma_start(out[0, b * P : (b + 1) * P, first:last], result[:])

@@ -32,7 +32,9 @@ LINE = 4
 HALF = SLOTS // 2
 EARLY_TOKENS = 512
 VECTOR_ZEROES = 1664
-STEPS = (((0, 128), (128, 256), (256, 512)), ((0, 128), (128, 256), (256, 384), (384, 512)))
+STEPS = (((0, 128), (128, 256), (256, 512)), ((0, 256), (256, 384), (384, 512)))
+BANKS = ((0, 1, 2), (3, 0, 1))
+VECTOR_ROWS = 64
 STORES = (((0, 256), (256, 512)), ((0, 384), (384, 512)))
 
 FLOPS = 2 * FEATURES * QUERIES * SLOTS
@@ -51,7 +53,7 @@ def tile_attend_capkb_kernel(tc, qT, k_words, k_scales, kb, offs, out):
         nc.sync.dma_start(offsets[:], offs)
 
         q_rows = qT[0].rearrange("(o p r) q -> o p r q", o=PASSES, r=PACK)
-        q_raw0 = sb.tile([P, PACK, QUERIES], F32, name="q_raw0")
+        q_raw0 = sb.tile([P, PACK, QUERIES], F32, name="q_raw0", align_bytes=64)
         q_raw1 = [sb.tile([P, PACK, P], F32, name=f"q_raw1{b}", align_bytes=64) for b in range(BLOCKS)]
         word_pool = sb.tile([P, TOKENS], I32, name="word_pool", align_bytes=64)
         word_rows = k_words[0].rearrange("p t b -> p (t b)").bitcast(I32)
@@ -78,7 +80,7 @@ def tile_attend_capkb_kernel(tc, qT, k_words, k_scales, kb, offs, out):
         bias_row = sb.tile([P, SLOTS], F32, name="bias_row", align_bytes=64)
         nc.vector.tensor_copy(bias_row[:], bias_pool[:].indirect(offsets[:]))
         slot_tiles = SLOTS // P
-        turned = ps.tile([P, slot_tiles, P], F32, name="turned", tag="scores1384")
+        turned = ps.tile([P, slot_tiles, P], F32, name="turned")
         for j in range(slot_tiles):
             nc.tensor.transpose(turned[:, j, :], bias_row[:, j * P : (j + 1) * P], ident[:])
         bias_cols = sb.tile([P, slot_tiles], F32, name="bias_cols")
@@ -97,7 +99,10 @@ def tile_attend_capkb_kernel(tc, qT, k_words, k_scales, kb, offs, out):
         halves = words[:].bitcast(U16).rearrange("p (n o) -> p o n", o=PASSES)
 
         scores = [
-            [ps.tile([P, stop - start], F32, name=f"scores{b}{start}") for start, stop in STEPS[b]]
+            [
+                ps.tile([P, stop - start], F32, name=f"scores{b}{start}", tag=f"bank{bank}")
+                for bank, (start, stop) in zip(BANKS[b], STEPS[b])
+            ]
             for b in range(BLOCKS)
         ]
 
@@ -106,12 +111,13 @@ def tile_attend_capkb_kernel(tc, qT, k_words, k_scales, kb, offs, out):
             nc.vector.tensor_copy(codes[:].bitcast(U16), halves[:, o, first:last])
             return [codes[:, 2 * n : 2 * (n + P)] for n in range(0, last - first, P)]
 
-        def interleave(name, raw, copy, tag):
-            grouped = sb.tile([P, P, PACK], BF16, name=name, tag=tag, align_bytes=64)
-            copy(
-                grouped[:].rearrange("p (c i) r -> p c r i", i=LINE),
-                raw.rearrange("p r (c i) -> p c r i", i=LINE),
-            )
+        def interleave(name, raw, shares):
+            grouped = sb.tile([P, P, PACK], BF16, name=name, align_bytes=64)
+            for copy, first, last in shares:
+                copy(
+                    grouped[:, first:last, :].rearrange("p (c i) r -> p c r i", i=LINE),
+                    raw[:, :, first:last].rearrange("p r (c i) -> p c r i", i=LINE),
+                )
             return grouped
 
         def quantize(name, grouped):
@@ -136,18 +142,23 @@ def tile_attend_capkb_kernel(tc, qT, k_words, k_scales, kb, offs, out):
                     stop=(o == PASSES - 1 and n + P == stop),
                 )
 
-        k_codes0 = part(0, 0, SLOTS, "k_codes0")
-        q00 = quantize("00", interleave("grouped00", q_raw0[:, :, 0:P], nc.scalar.copy, "grouped00"))
+        scalar_alone = [(nc.scalar.copy, 0, P)]
+        shared = [(nc.vector.tensor_copy, 0, VECTOR_ROWS), (nc.scalar.copy, VECTOR_ROWS, P)]
+        k_codes0 = part(0, 0, HALF, "k_codes0")
+        q00 = quantize("00", interleave("grouped00", q_raw0[:, :, 0:P], scalar_alone))
+        k_codes0 = k_codes0 + part(0, HALF, SLOTS, "grouped00")
         for step in range(len(STEPS[0])):
             multiply(0, 0, step, q00, k_codes0)
-        k_codes1 = part(1, 0, SLOTS, "grouped00")
-        q10 = quantize("10", interleave("grouped10", q_raw1[0][:], nc.scalar.copy, "grouped10"))
+        q01 = quantize("01", interleave("grouped01", q_raw0[:, :, P:QUERIES], shared))
+        multiply(0, 1, 0, q01, k_codes0)
+        k_codes1 = part(1, 0, HALF, "q_raw0")
+        q10 = quantize("10", interleave("grouped10", q_raw1[0], scalar_alone))
+        k_codes1 = k_codes1 + part(1, HALF, SLOTS, "q_raw10")
         for step in range(len(STEPS[0])):
             multiply(1, 0, step, q10, k_codes1)
-        grouped11 = interleave("grouped11", q_raw1[1][:], nc.vector.tensor_copy, "q_raw10")
-        q01 = quantize("01", interleave("grouped01", q_raw0[:, :, P:QUERIES], nc.scalar.copy, "grouped01"))
-        q11 = quantize("11", grouped11)
-        for step in range(len(STEPS[1])):
+        q11 = quantize("11", interleave("grouped11", q_raw1[1], scalar_alone))
+        multiply(1, 1, 0, q11, k_codes1)
+        for step in range(1, len(STEPS[1])):
             multiply(0, 1, step, q01, k_codes0)
             multiply(1, 1, step, q11, k_codes1)
 

@@ -49,8 +49,6 @@ def tile_attend_capkb_kernel(tc, qT, k_words, k_scales, kb, offs, out):
 
         offsets = sb.tile([P, SLOTS // 16], U16, name="offsets")
         bias_pool = sb.tile([P, TOKENS], F32, name="bias_pool", align_bytes=64)
-        nc.sync.dma_start(bias_pool[BIAS_ROW:P, :], kb[0:1, :])
-        nc.sync.dma_start(offsets[:], offs)
 
         q_rows = qT[0].rearrange("(o p r) q -> o p r q", o=PASSES, r=PACK)
         q_raw0 = sb.tile([P, PACK, QUERIES], F32, name="q_raw0", align_bytes=64)
@@ -58,6 +56,8 @@ def tile_attend_capkb_kernel(tc, qT, k_words, k_scales, kb, offs, out):
         word_pool = sb.tile([P, TOKENS], I32, name="word_pool", align_bytes=64)
         word_rows = k_words[0].rearrange("p t b -> p (t b)").bitcast(I32)
         nc.sync.dma_start(word_pool[:, 0:EARLY_TOKENS], word_rows[:, 0:EARLY_TOKENS])
+        nc.sync.dma_start(bias_pool[BIAS_ROW:P, :], kb[0:1, :])
+        nc.sync.dma_start(offsets[:], offs)
 
         scale_pool = sb.tile([P, TOKENS], U8, name="scale_pool", align_bytes=64)
         nc.gpsimd.memset(scale_pool[:].bitcast(I32), 0)

@@ -31,7 +31,6 @@ BIAS_ROW = P - 1
 LINE = 4
 HALF = SLOTS // 2
 EARLY_TOKENS = 512
-VECTOR_ZEROES = 1664
 STEPS = (((0, 128), (128, 256), (256, 512)), ((0, 256), (256, 384), (384, 512)))
 BANKS = ((0, 1, 2), (3, 0, 1))
 VECTOR_ROWS = 64
@@ -72,8 +71,7 @@ def tile_attend_capkb_kernel(tc, qT, k_words, k_scales, kb, offs, out):
 
         k_scale1 = sb.tile([P, SLOTS], U8, name="k_scale1", align_bytes=64)
         ident = sb.tile([P, P], F32, name="ident")
-        nc.vector.memset(bias_pool[0:BIAS_ROW, 0:VECTOR_ZEROES].bitcast(I32), 0)
-        nc.gpsimd.memset(bias_pool[0:BIAS_ROW, VECTOR_ZEROES:TOKENS].bitcast(I32), 0)
+        nc.vector.memset(bias_pool[0:BIAS_ROW, :].bitcast(I32), 0)
         make_identity(nc, ident[:])
         nc.gpsimd.memset(k_scale1[:].bitcast(I32), 0)
 

@@ -34,7 +34,7 @@ EARLY_TOKENS = 512
 STEPS = (((0, 128), (128, 256), (256, 512)), ((0, 256), (256, 384), (384, 512)))
 BANKS = ((0, 1, 2), (3, 0, 1))
 VECTOR_ROWS = 64
-STORES = (((0, 256), (256, 512)), ((0, 384), (384, 512)))
+STORES = (((0, 256), (256, 512)), ((0, 256), (256, 512)))
 
 FLOPS = 2 * FEATURES * QUERIES * SLOTS
 BYTES = 4 * FEATURES * QUERIES + 4 * P * TOKENS + 32 * TOKENS + 4 * TOKENS + 2 * P * SLOTS // 16 + 4 * QUERIES * SLOTS

@@ -126,6 +126,23 @@ def tile_attend_capkb_kernel(tc, qT, k_words, k_scales, kb, offs, out):
             )
             return q_codes, q_scale
 
+        def quantize_in_halves(name, raw, tag):
+            q_codes = sb.tile([P, P], U32, name=f"q_codes{name}", align_bytes=64)
+            q_scale = sb.tile([P, P], U8, name=f"q_scale{name}", align_bytes=64)
+            rows = P // 2
+            for first, copy, buffer in ((rows, nc.scalar.copy, f"grouped{name}"), (0, nc.vector.tensor_copy, tag)):
+                grouped = sb.tile([P, rows, PACK], BF16, name=f"grouped{name}{first}", tag=buffer, align_bytes=64)
+                copy(
+                    grouped[:].rearrange("p (c i) r -> p c r i", i=LINE),
+                    raw[:, :, first : first + rows].rearrange("p r (c i) -> p c r i", i=LINE),
+                )
+                nc.vector.quantize_mx(
+                    out=q_codes[:, first : first + rows].bitcast(FP8X4),
+                    scales=q_scale[:, first : first + rows],
+                    in_=grouped[:].rearrange("p q r -> p (q r)"),
+                )
+            return q_codes, q_scale
+
         def multiply(o, b, step, quantized, k_codes):
             q_codes, q_scale = quantized
             start, stop = STEPS[b][step]
@@ -149,12 +166,11 @@ def tile_attend_capkb_kernel(tc, qT, k_words, k_scales, kb, offs, out):
             multiply(0, 0, step, q00, k_codes0)
         q01 = quantize("01", interleave("grouped01", q_raw0[:, :, P:QUERIES], shared))
         multiply(0, 1, 0, q01, k_codes0)
-        k_codes1 = part(1, 0, HALF, "q_raw0")
+        k_codes1 = part(1, 0, SLOTS, "q_raw0")
         q10 = quantize("10", interleave("grouped10", q_raw1[0], scalar_alone))
-        k_codes1 = k_codes1 + part(1, HALF, SLOTS, "q_raw10")
         for step in range(len(STEPS[0])):
             multiply(1, 0, step, q10, k_codes1)
-        q11 = quantize("11", interleave("grouped11", q_raw1[1], scalar_alone))
+        q11 = quantize_in_halves("11", q_raw1[1], "q_raw10")
         multiply(1, 1, 0, q11, k_codes1)
         for step in range(1, len(STEPS[1])):
             multiply(0, 1, step, q01, k_codes0)

@@ -31,8 +31,8 @@ BIAS_ROW = P - 1
 LINE = 4
 HALF = SLOTS // 2
 EARLY_TOKENS = 512
-STEPS = (((0, 128), (128, 256), (256, 512)), ((0, 256), (256, 384), (384, 512)))
-BANKS = ((0, 1, 2), (3, 0, 1))
+STEPS = (((0, 128), (128, 256), (256, 384), (384, 512)),) * BLOCKS
+BANKS = ((0, 1, 2, 3), (4, 5, 0, 1))
 VECTOR_ROWS = 64
 STORES = (((0, 256), (256, 512)), ((0, 256), (256, 512)))
 
@@ -166,13 +166,15 @@ def tile_attend_capkb_kernel(tc, qT, k_words, k_scales, kb, offs, out):
             multiply(0, 0, step, q00, k_codes0)
         q01 = quantize("01", interleave("grouped01", q_raw0[:, :, P:QUERIES], shared))
         multiply(0, 1, 0, q01, k_codes0)
+        multiply(0, 1, 1, q01, k_codes0)
         k_codes1 = part(1, 0, SLOTS, "q_raw0")
         q10 = quantize("10", interleave("grouped10", q_raw1[0], scalar_alone))
         for step in range(len(STEPS[0])):
             multiply(1, 0, step, q10, k_codes1)
         q11 = quantize_in_halves("11", q_raw1[1], "q_raw10")
         multiply(1, 1, 0, q11, k_codes1)
-        for step in range(1, len(STEPS[1])):
+        multiply(1, 1, 1, q11, k_codes1)
+        for step in range(2, len(STEPS[1])):
             multiply(0, 1, step, q01, k_codes0)
             multiply(1, 1, step, q11, k_codes1)
 

@@ -34,6 +34,7 @@ EARLY_TOKENS = 512
 STEPS = (((0, 128), (128, 256), (256, 384), (384, 512)),) * BLOCKS
 BANKS = ((0, 1, 2, 3), (4, 5, 0, 1))
 VECTOR_ROWS = 64
+ODD_SPLIT = TOKENS // 2 + 1
 STORES = (((0, 256), (256, 512)), ((0, 256), (256, 512)))
 
 FLOPS = 2 * FEATURES * QUERIES * SLOTS
@@ -71,7 +72,8 @@ def tile_attend_capkb_kernel(tc, qT, k_words, k_scales, kb, offs, out):
 
         k_scale1 = sb.tile([P, SLOTS], U8, name="k_scale1", align_bytes=64)
         ident = sb.tile([P, P], F32, name="ident")
-        nc.vector.memset(bias_pool[0:BIAS_ROW, :].bitcast(I32), 0)
+        nc.vector.memset(bias_pool[0:BIAS_ROW, 0:ODD_SPLIT].bitcast(I32), 0)
+        nc.vector.memset(bias_pool[0:BIAS_ROW, ODD_SPLIT:TOKENS].bitcast(I32), 0)
         make_identity(nc, ident[:])
         nc.gpsimd.memset(k_scale1[:].bitcast(I32), 0)
 

@@ -162,11 +162,11 @@ def tile_attend_capkb_kernel(tc, qT, k_words, k_scales, kb, offs, out):
         scalar_alone = [(nc.scalar.copy, 0, P)]
         shared = [(nc.vector.tensor_copy, 0, VECTOR_ROWS), (nc.scalar.copy, VECTOR_ROWS, P)]
         k_codes0 = part(0, 0, HALF, "k_codes0")
-        q00 = quantize("00", interleave("grouped00", q_raw0[:, :, 0:P], scalar_alone))
+        q00 = quantize("00", interleave("grouped00", q_raw0[:, :, 0:P], shared))
         k_codes0 = k_codes0 + part(0, HALF, SLOTS, "grouped00")
         for step in range(len(STEPS[0])):
             multiply(0, 0, step, q00, k_codes0)
-        q01 = quantize("01", interleave("grouped01", q_raw0[:, :, P:QUERIES], shared))
+        q01 = quantize("01", interleave("grouped01", q_raw0[:, :, P:QUERIES], scalar_alone))
         multiply(0, 1, 0, q01, k_codes0)
         multiply(0, 1, 1, q01, k_codes0)
         k_codes1 = part(1, 0, SLOTS, "q_raw0")

@@ -32,7 +32,7 @@ LINE = 4
 HALF = SLOTS // 2
 EARLY_TOKENS = 512
 STEPS = (((0, 128), (128, 256), (256, 384), (384, 512)),) * BLOCKS
-BANKS = ((0, 1, 2, 3), (4, 5, 0, 1))
+BANKS = ((0, 1, 2, 3), (4, 5, 6, 0))
 VECTOR_ROWS = 64
 ODD_SPLIT = TOKENS // 2 + 1
 STORES = (((0, 256), (256, 512)), ((0, 256), (256, 512)))
@@ -80,7 +80,7 @@ def tile_attend_capkb_kernel(tc, qT, k_words, k_scales, kb, offs, out):
         bias_row = sb.tile([P, SLOTS], F32, name="bias_row", align_bytes=64)
         nc.vector.tensor_copy(bias_row[:], bias_pool[:].indirect(offsets[:]))
         slot_tiles = SLOTS // P
-        turned = ps.tile([P, slot_tiles, P], F32, name="turned")
+        turned = ps.tile([P, slot_tiles, P], F32, name="turned", tag="bank6")
         for j in range(slot_tiles):
             nc.tensor.transpose(turned[:, j, :], bias_row[:, j * P : (j + 1) * P], ident[:])
         bias_cols = sb.tile([P, slot_tiles], F32, name="bias_cols")
@@ -163,20 +163,22 @@ def tile_attend_capkb_kernel(tc, qT, k_words, k_scales, kb, offs, out):
         shared = [(nc.vector.tensor_copy, 0, VECTOR_ROWS), (nc.scalar.copy, VECTOR_ROWS, P)]
         k_codes0 = part(0, 0, HALF, "k_codes0")
         q00 = quantize("00", interleave("grouped00", q_raw0[:, :, 0:P], shared))
-        k_codes0 = k_codes0 + part(0, HALF, SLOTS, "grouped00")
+        k_codes0 = k_codes0 + part(0, HALF, SLOTS, "q_raw0")
         for step in range(len(STEPS[0])):
             multiply(0, 0, step, q00, k_codes0)
-        q01 = quantize("01", interleave("grouped01", q_raw0[:, :, P:QUERIES], scalar_alone))
+        q01 = quantize("01", interleave("grouped01", q_raw0[:, :, P:QUERIES], shared))
         multiply(0, 1, 0, q01, k_codes0)
         multiply(0, 1, 1, q01, k_codes0)
-        k_codes1 = part(1, 0, SLOTS, "q_raw0")
+        multiply(0, 1, 2, q01, k_codes0)
+        k_codes1 = part(1, 0, SLOTS, "grouped00")
         q10 = quantize("10", interleave("grouped10", q_raw1[0], scalar_alone))
         for step in range(len(STEPS[0])):
             multiply(1, 0, step, q10, k_codes1)
         q11 = quantize_in_halves("11", q_raw1[1], "q_raw10")
         multiply(1, 1, 0, q11, k_codes1)
         multiply(1, 1, 1, q11, k_codes1)
-        for step in range(2, len(STEPS[1])):
+        multiply(1, 1, 2, q11, k_codes1)
+        for step in range(3, len(STEPS[1])):
             multiply(0, 1, step, q01, k_codes0)
             multiply(1, 1, step, q11, k_codes1)
 

@@ -30,11 +30,11 @@ SHIFT = 16
 BIAS_ROW = P - 1
 LINE = 4
 HALF = SLOTS // 2
-EARLY_TOKENS = 512
+EARLY_TOKENS = 384
 STEPS = (((0, 128), (128, 256), (256, 384), (384, 512)),) * BLOCKS
 BANKS = ((0, 1, 2, 3), (4, 5, 6, 0))
 VECTOR_ROWS = 64
-ODD_SPLIT = TOKENS // 2 + 1
+VECTOR_ZEROES = 1664
 STORES = (((0, 256), (256, 512)), ((0, 256), (256, 512)))
 
 FLOPS = 2 * FEATURES * QUERIES * SLOTS
@@ -46,6 +46,12 @@ def tile_attend_capkb_kernel(tc, qT, k_words, k_scales, kb, offs, out):
     with ExitStack() as ctx:
         sb = ctx.enter_context(tc.tile_pool(name="sb", bufs=1))
         ps = ctx.enter_context(tc.psum_pool(name="ps", bufs=1))
+
+        def zero_together(words, vector_words):
+            odd = vector_words // 2 + 1
+            nc.vector.memset(words[:, 0:odd], 0)
+            nc.vector.memset(words[:, odd:vector_words], 0)
+            nc.gpsimd.memset(words[:, vector_words:], 0)
 
         offsets = sb.tile([P, SLOTS // 16], U16, name="offsets")
         bias_pool = sb.tile([P, TOKENS], F32, name="bias_pool", align_bytes=64)
@@ -60,7 +66,7 @@ def tile_attend_capkb_kernel(tc, qT, k_words, k_scales, kb, offs, out):
         nc.sync.dma_start(offsets[:], offs)
 
         scale_pool = sb.tile([P, TOKENS], U8, name="scale_pool", align_bytes=64)
-        nc.gpsimd.memset(scale_pool[:].bitcast(I32), 0)
+        zero_together(scale_pool[:].bitcast(I32), TOKENS // 8)
         scale_rows = k_scales.bitcast(I32).rearrange("o (c r) t -> r c o t", r=SCALE_ROWS)
         for r in range(SCALE_ROWS):
             nc.sync.dma_start(scale_pool[r:P:SHIFT, :].bitcast(I32), scale_rows[r])
@@ -72,8 +78,7 @@ def tile_attend_capkb_kernel(tc, qT, k_words, k_scales, kb, offs, out):
 
         k_scale1 = sb.tile([P, SLOTS], U8, name="k_scale1", align_bytes=64)
         ident = sb.tile([P, P], F32, name="ident")
-        nc.vector.memset(bias_pool[0:BIAS_ROW, 0:ODD_SPLIT].bitcast(I32), 0)
-        nc.vector.memset(bias_pool[0:BIAS_ROW, ODD_SPLIT:TOKENS].bitcast(I32), 0)
+        zero_together(bias_pool[0:BIAS_ROW, :].bitcast(I32), VECTOR_ZEROES)
         make_identity(nc, ident[:])
         nc.gpsimd.memset(k_scale1[:].bitcast(I32), 0)
 
@@ -95,7 +100,9 @@ def tile_attend_capkb_kernel(tc, qT, k_words, k_scales, kb, offs, out):
         k_scale = [k_scale0, k_scale1]
 
         words = sb.tile([P, SLOTS], U32, name="words", align_bytes=64)
-        nc.vector.tensor_copy(words[:], word_pool[:].bitcast(U32).indirect(offsets[:]))
+        for first in (0, HALF):
+            listed = offsets[:, first // 16 : (first + HALF) // 16]
+            nc.vector.tensor_copy(words[:, first : first + HALF], word_pool[:].bitcast(U32).indirect(listed))
         halves = words[:].bitcast(U16).rearrange("p (n o) -> p o n", o=PASSES)
 
         scores = [

@@ -33,7 +33,7 @@ HALF = SLOTS // 2
 EARLY_TOKENS = 384
 STEPS = (((0, 128), (128, 256), (256, 384), (384, 512)),) * BLOCKS
 BANKS = ((0, 1, 2, 3), (4, 5, 6, 0))
-VECTOR_ROWS = 64
+VECTOR_ROWS = 96
 VECTOR_ZEROES = 1664
 STORES = (((0, 256), (256, 512)), ((0, 256), (256, 512)))
 

@@ -30,7 +30,7 @@ SHIFT = 16
 BIAS_ROW = P - 1
 LINE = 4
 HALF = SLOTS // 2
-EARLY_TOKENS = 384
+EARLY_TOKENS = 1024
 STEPS = (((0, 128), (128, 256), (256, 384), (384, 512)),) * BLOCKS
 BANKS = ((0, 1, 2, 3), (4, 5, 6, 0))
 VECTOR_ROWS = 96
@@ -65,6 +65,11 @@ def tile_attend_capkb_kernel(tc, qT, k_words, k_scales, kb, offs, out):
         nc.sync.dma_start(bias_pool[BIAS_ROW:P, :], kb[0:1, :])
         nc.sync.dma_start(offsets[:], offs)
 
+        column = sb.tile([P, 1], F32, name="column")
+        unread = sb.tile([P, 1], F32, name="unread")
+        nc.gpsimd.memset(column[:], 0.0)
+        nc.scalar.activation(unread[:], column[:], TANH)
+
         scale_pool = sb.tile([P, TOKENS], U8, name="scale_pool", align_bytes=64)
         zero_together(scale_pool[:].bitcast(I32), TOKENS // 8)
         scale_rows = k_scales.bitcast(I32).rearrange("o (c r) t -> r c o t", r=SCALE_ROWS)
@@ -83,7 +88,7 @@ def tile_attend_capkb_kernel(tc, qT, k_words, k_scales, kb, offs, out):
         nc.gpsimd.memset(k_scale1[:].bitcast(I32), 0)
 
         bias_row = sb.tile([P, SLOTS], F32, name="bias_row", align_bytes=64)
-        nc.vector.tensor_copy(bias_row[:], bias_pool[:].indirect(offsets[:]))
+        nc.scalar.activation(bias_row[:], bias_pool[:].indirect(offsets[:]), COPY)
         slot_tiles = SLOTS // P
         turned = ps.tile([P, slot_tiles, P], F32, name="turned", tag="bank6")
         for j in range(slot_tiles):

@@ -30,7 +30,7 @@ SHIFT = 16
 BIAS_ROW = P - 1
 LINE = 4
 HALF = SLOTS // 2
-EARLY_TOKENS = 1024
+EARLY_TOKENS = 576
 STEPS = (((0, 128), (128, 256), (256, 384), (384, 512)),) * BLOCKS
 BANKS = ((0, 1, 2, 3), (4, 5, 6, 0))
 VECTOR_ROWS = 96
@@ -65,16 +65,16 @@ def tile_attend_capkb_kernel(tc, qT, k_words, k_scales, kb, offs, out):
         nc.sync.dma_start(bias_pool[BIAS_ROW:P, :], kb[0:1, :])
         nc.sync.dma_start(offsets[:], offs)
 
-        column = sb.tile([P, 1], F32, name="column")
-        unread = sb.tile([P, 1], F32, name="unread")
-        nc.gpsimd.memset(column[:], 0.0)
-        nc.scalar.activation(unread[:], column[:], TANH)
-
         scale_pool = sb.tile([P, TOKENS], U8, name="scale_pool", align_bytes=64)
         zero_together(scale_pool[:].bitcast(I32), TOKENS // 8)
         scale_rows = k_scales.bitcast(I32).rearrange("o (c r) t -> r c o t", r=SCALE_ROWS)
         for r in range(SCALE_ROWS):
             nc.sync.dma_start(scale_pool[r:P:SHIFT, :].bitcast(I32), scale_rows[r])
+
+        column = sb.tile([P, 1], F32, name="column")
+        unread = sb.tile([P, 1], F32, name="unread")
+        nc.gpsimd.memset(column[:], 0.0)
+        nc.scalar.activation(unread[:], column[:], TANH)
 
         nc.sync.dma_start(word_pool[:, EARLY_TOKENS:TOKENS], word_rows[:, EARLY_TOKENS:TOKENS])
         nc.sync.dma_start(q_raw0[:], q_rows[0])

from contextlib import ExitStack

import concourse.mybir as mybir
from concourse.masks import make_identity

F32 = mybir.dt.float32
BF16 = mybir.dt.bfloat16
I32 = mybir.dt.int32
U32 = mybir.dt.uint32
U16 = mybir.dt.uint16
U8 = mybir.dt.uint8
FP8X4 = mybir.dt.float8_e4m3fn_x4
FP4X4 = mybir.dt.float4_e2m1fn_x4
TANH = mybir.ActivationFunctionType.Tanh
COPY = mybir.ActivationFunctionType.Copy
MULT = mybir.AluOpType.mult
ADD = mybir.AluOpType.add

P = 128
PACK = 4
PASSES = 2
BLOCKS = 2
SLOTS = 512
TOKENS = 2048
FEATURES = PASSES * PACK * P
QUERIES = BLOCKS * P
CAP = 30.0
SCALE_ROWS = 4
SHIFT = 16
BIAS_ROW = P - 1
LINE = 4
HALF = SLOTS // 2
EARLY_TOKENS = 576
STEPS = (((0, 128), (128, 256), (256, 384), (384, 512)),) * BLOCKS
BANKS = ((0, 1, 2, 3), (4, 5, 6, 0))
VECTOR_ROWS = 96
VECTOR_ZEROES = 1664
STORES = (((0, 256), (256, 512)), ((0, 256), (256, 512)))

FLOPS = 2 * FEATURES * QUERIES * SLOTS
BYTES = 4 * FEATURES * QUERIES + 4 * P * TOKENS + 32 * TOKENS + 4 * TOKENS + 2 * P * SLOTS // 16 + 4 * QUERIES * SLOTS


def tile_attend_capkb_kernel(tc, qT, k_words, k_scales, kb, offs, out):
    nc = tc.nc
    with ExitStack() as ctx:
        sb = ctx.enter_context(tc.tile_pool(name="sb", bufs=1))
        ps = ctx.enter_context(tc.psum_pool(name="ps", bufs=1))

        def zero_together(words, vector_words):
            odd = vector_words // 2 + 1
            nc.vector.memset(words[:, 0:odd], 0)
            nc.vector.memset(words[:, odd:vector_words], 0)
            nc.gpsimd.memset(words[:, vector_words:], 0)

        offsets = sb.tile([P, SLOTS // 16], U16, name="offsets")
        bias_pool = sb.tile([P, TOKENS], F32, name="bias_pool", align_bytes=64)

        q_rows = qT[0].rearrange("(o p r) q -> o p r q", o=PASSES, r=PACK)
        q_raw0 = sb.tile([P, PACK, QUERIES], F32, name="q_raw0", align_bytes=64)
        q_raw1 = [sb.tile([P, PACK, P], F32, name=f"q_raw1{b}", align_bytes=64) for b in range(BLOCKS)]
        word_pool = sb.tile([P, TOKENS], I32, name="word_pool", align_bytes=64)
        word_rows = k_words[0].rearrange("p t b -> p (t b)").bitcast(I32)
        nc.sync.dma_start(word_pool[:, 0:EARLY_TOKENS], word_rows[:, 0:EARLY_TOKENS])
        nc.sync.dma_start(bias_pool[BIAS_ROW:P, :], kb[0:1, :])
        nc.sync.dma_start(offsets[:], offs)

        scale_pool = sb.tile([P, TOKENS], U8, name="scale_pool", align_bytes=64)
        zero_together(scale_pool[:].bitcast(I32), TOKENS // 8)
        scale_rows = k_scales.bitcast(I32).rearrange("o (c r) t -> r c o t", r=SCALE_ROWS)
        for r in range(SCALE_ROWS):
            nc.sync.dma_start(scale_pool[r:P:SHIFT, :].bitcast(I32), scale_rows[r])

        column = sb.tile([P, 1], F32, name="column")
        unread = sb.tile([P, 1], F32, name="unread")
        nc.gpsimd.memset(column[:], 0.0)
        nc.scalar.activation(unread[:], column[:], TANH)

        nc.sync.dma_start(word_pool[:, EARLY_TOKENS:TOKENS], word_rows[:, EARLY_TOKENS:TOKENS])
        nc.sync.dma_start(q_raw0[:], q_rows[0])
        for b in range(BLOCKS):
            nc.sync.dma_start(q_raw1[b][:], q_rows[1][:, :, b * P : (b + 1) * P])

        k_scale1 = sb.tile([P, SLOTS], U8, name="k_scale1", align_bytes=64)
        ident = sb.tile([P, P], F32, name="ident")
        zero_together(bias_pool[0:BIAS_ROW, :].bitcast(I32), VECTOR_ZEROES)
        make_identity(nc, ident[:])
        nc.gpsimd.memset(k_scale1[:].bitcast(I32), 0)

        bias_row = sb.tile([P, SLOTS], F32, name="bias_row", align_bytes=64)
        nc.scalar.activation(bias_row[:], bias_pool[:].indirect(offsets[:]), COPY)
        slot_tiles = SLOTS // P
        turned = ps.tile([P, slot_tiles, P], F32, name="turned", tag="bank6")
        for j in range(slot_tiles):
            nc.tensor.transpose(turned[:, j, :], bias_row[:, j * P : (j + 1) * P], ident[:])
        bias_cols = sb.tile([P, slot_tiles], F32, name="bias_cols")
        nc.scalar.activation(bias_cols[:], turned[:, :, BIAS_ROW], COPY)
        bias = ps.tile([P, SLOTS], F32, name="bias")
        for j in range(slot_tiles):
            nc.tensor.transpose(bias[:, j * P : (j + 1) * P], bias_cols[:, j : j + 1].to_broadcast([P, P]), ident[:])

        k_scale0 = sb.tile([P, SLOTS], U8, name="k_scale0", align_bytes=64)
        nc.vector.tensor_copy(k_scale0[:], scale_pool[:].indirect(offsets[:]))
        nc.sync.dma_start(k_scale1[0 : P - SHIFT, :].bitcast(I32), k_scale0[SHIFT:P, :].bitcast(I32))
        k_scale = [k_scale0, k_scale1]

        words = sb.tile([P, SLOTS], U32, name="words", align_bytes=64)
        for first in (0, HALF):
            listed = offsets[:, first // 16 : (first + HALF) // 16]
            nc.vector.tensor_copy(words[:, first : first + HALF], word_pool[:].bitcast(U32).indirect(listed))
        halves = words[:].bitcast(U16).rearrange("p (n o) -> p o n", o=PASSES)

        scores = [
            [
                ps.tile([P, stop - start], F32, name=f"scores{b}{start}", tag=f"bank{bank}")
                for bank, (start, stop) in zip(BANKS[b], STEPS[b])
            ]
            for b in range(BLOCKS)
        ]

        def part(o, first, last, tag):
            codes = sb.tile([P, 2 * (last - first)], U8, name=f"k_codes{o}{first}", tag=tag, align_bytes=64)
            nc.vector.tensor_copy(codes[:].bitcast(U16), halves[:, o, first:last])
            return [codes[:, 2 * n : 2 * (n + P)] for n in range(0, last - first, P)]

        def interleave(name, raw, shares):
            grouped = sb.tile([P, P, PACK], BF16, name=name, align_bytes=64)
            for copy, first, last in shares:
                copy(
                    grouped[:, first:last, :].rearrange("p (c i) r -> p c r i", i=LINE),
                    raw[:, :, first:last].rearrange("p r (c i) -> p c r i", i=LINE),
                )
            return grouped

        def quantize(name, grouped):
            q_codes = sb.tile([P, P], U32, name=f"q_codes{name}", align_bytes=64)
            q_scale = sb.tile([P, P], U8, name=f"q_scale{name}", align_bytes=64)
            nc.vector.quantize_mx(
                out=q_codes[:].bitcast(FP8X4), scales=q_scale[:], in_=grouped[:].rearrange("p q r -> p (q r)")
            )
            return q_codes, q_scale

        def quantize_in_halves(name, raw, tag):
            q_codes = sb.tile([P, P], U32, name=f"q_codes{name}", align_bytes=64)
            q_scale = sb.tile([P, P], U8, name=f"q_scale{name}", align_bytes=64)
            rows = P // 2
            for first, copy, buffer in ((rows, nc.scalar.copy, f"grouped{name}"), (0, nc.vector.tensor_copy, tag)):
                grouped = sb.tile([P, rows, PACK], BF16, name=f"grouped{name}{first}", tag=buffer, align_bytes=64)
                copy(
                    grouped[:].rearrange("p (c i) r -> p c r i", i=LINE),
                    raw[:, :, first : first + rows].rearrange("p r (c i) -> p c r i", i=LINE),
                )
                nc.vector.quantize_mx(
                    out=q_codes[:, first : first + rows].bitcast(FP8X4),
                    scales=q_scale[:, first : first + rows],
                    in_=grouped[:].rearrange("p q r -> p (q r)"),
                )
            return q_codes, q_scale

        def multiply(o, b, step, quantized, k_codes):
            q_codes, q_scale = quantized
            start, stop = STEPS[b][step]
            for n in range(start, stop, P):
                nc.tensor.matmul_mx(
                    out=scores[b][step][:, n - start : n - start + P],
                    lhsT=q_codes[:].bitcast(FP8X4),
                    lhsT_scale=q_scale[:],
                    rhs=k_codes[n // P].bitcast(FP4X4),
                    rhs_scale=k_scale[o][:, n : n + P],
                    start=(o == 0 and n == start),
                    stop=(o == PASSES - 1 and n + P == stop),
                )

        scalar_alone = [(nc.scalar.copy, 0, P)]
        shared = [(nc.vector.tensor_copy, 0, VECTOR_ROWS), (nc.scalar.copy, VECTOR_ROWS, P)]
        k_codes0 = part(0, 0, HALF, "k_codes0")
        q00 = quantize("00", interleave("grouped00", q_raw0[:, :, 0:P], shared))
        k_codes0 = k_codes0 + part(0, HALF, SLOTS, "q_raw0")
        for step in range(len(STEPS[0])):
            multiply(0, 0, step, q00, k_codes0)
        q01 = quantize("01", interleave("grouped01", q_raw0[:, :, P:QUERIES], shared))
        multiply(0, 1, 0, q01, k_codes0)
        multiply(0, 1, 1, q01, k_codes0)
        multiply(0, 1, 2, q01, k_codes0)
        k_codes1 = part(1, 0, SLOTS, "grouped00")
        q10 = quantize("10", interleave("grouped10", q_raw1[0], scalar_alone))
        for step in range(len(STEPS[0])):
            multiply(1, 0, step, q10, k_codes1)
        q11 = quantize_in_halves("11", q_raw1[1], "q_raw10")
        multiply(1, 1, 0, q11, k_codes1)
        multiply(1, 1, 1, q11, k_codes1)
        multiply(1, 1, 2, q11, k_codes1)
        for step in range(3, len(STEPS[1])):
            multiply(0, 1, step, q01, k_codes0)
            multiply(1, 1, step, q11, k_codes1)

        for b in range(BLOCKS):
            results = [sb.tile([P, last - first], F32, name=f"result{b}{first}") for first, last in STORES[b]]
            for bank, (start, stop) in zip(scores[b], STEPS[b]):
                capped = sb.tile([P, stop - start], F32, name=f"capped{b}{start}")
                nc.scalar.activation(capped[:], bank[:], TANH, scale=1.0 / CAP)
                for result, (first, last) in zip(results, STORES[b]):
                    if first <= start < last:
                        nc.vector.scalar_tensor_tensor(
                            result[:, start - first : stop - first], capped[:], CAP, bias[:, start:stop], MULT, ADD
                        )
                        if stop == last:
                            nc.sync.dma_start(out[0, b * P : (b + 1) * P, first:last], result[:])
